import numpy as np, ml_dtypes
CORES = [40,64,80,88,96,104,120,144]
N = 8
import mx_ref
BF = ml_dtypes.bfloat16
def pick(q, e):
    c = np.concatenate([q[0].reshape(128, -1, 4), np.zeros((128, 1, 4), np.uint8)], axis=1); s = np.concatenate([q[1], np.ones((16, 1), np.uint8)], axis=1)
    return (np.ascontiguousarray(c[:, e].reshape(128, -1)), np.ascontiguousarray(s[:, e]))
def join(*qs):
    return (np.concatenate([q[0] for q in qs], axis=1), np.concatenate([q[1] for q in qs], axis=1))
def put(q, e, v):
    c, s = q[0].reshape(128, -1, 4).copy(), q[1].copy(); c[:, e] = v[0].reshape(128, -1, 4); s[:, e] = v[1]
    return (c.reshape(128, -1), s)
def pk(c, s):
    return (np.ascontiguousarray(c), mx_ref.live(s))
def emit(q):
    return q[0], q[1]
def decode(q):
    o = []
    for b in range(4):
        e = np.zeros((128, 128, 4), np.float32); e[np.arange(128), np.arange(128), b] = 1
        o.append(mx_ref.matmul(mx_ref.quantize(e.reshape(128, 512).astype(BF)), q))
    return np.stack(o, axis=2).reshape(128, -1)
def cut(t, i, w=512):
    return t[:, w * i:w * i + w]
def f(rng, *shape):
    return mx_ref.flush((rng.standard_normal(shape, dtype=np.float32) * np.exp2(rng.integers(-2, 3, shape[:-1] + (1,)))).astype(BF))
def wide(rng, *shape, cols=0):
    v = rng.standard_normal(shape, dtype=np.float32) * np.exp2(rng.integers(-12, 13, shape)).astype(np.float32)
    if cols: v *= np.repeat(np.exp2(rng.integers(-cols, cols + 1, shape[:-2] + (1, shape[-1] // 4))) * (rng.random(shape[:-2] + (1, shape[-1] // 4)) > 0.0625), 4, axis=-1).astype(np.float32)
    return mx_ref.flush(v.astype(BF))
C, T, M, R, G, O = 16, 128, 8, 3, 4, 2
def big(v):
    v = v.astype(np.float32)
    return np.where(np.abs(v) < np.float32(2.0 ** -16), np.float32(0), v).astype(BF)
def signed(rng, *shape):
    return (1 + rng.random(shape)) * rng.choice([-1.0, 1.0], shape)
def tiles(v):
    return np.ascontiguousarray(v.reshape(N, 128, -1).astype(np.float32).astype(BF))
def setup_inputs(rng):
    return {"c": big(f(rng, N, 128, 4 * C)), "x": big(f(rng, N, 128, 4 * T)), "u": f(rng, N, 128, 16), "w": f(rng, N, 128, 512 * O)}
def setup_inputs_dark(rng):
    d = setup_inputs(rng)
    top = np.arange(128) < 64
    kind = np.stack([rng.permutation(T) for r in range(N)]) < 2 * T // 3
    on = kind[:, None, :] == top[None, :, None]
    d["x"] = tiles((1.75 + 0.25 * rng.random((N, 128, T, 4))) * on[:, :, :, None] * 2.0 ** 29)
    d["u"] = tiles((2 + 0.2 * rng.random((N, 128, 4, 4))) * 2.0 ** 28)
    c = 0.5 * signed(rng, N * C, 128, 4)
    b = M + rng.permutation(N * C - M)[:2 * M]
    for half, e in ((top, b[:M + M // 2]), (~top, b[M + M // 2:])):
        c[np.ix_(e, np.flatnonzero(half))] = 2.5 + 0.5 * rng.random((len(e), 64, 4))
    d["c"] = tiles(c.reshape(N, C, 128, 4).transpose(0, 2, 1, 3) * 2.0 ** 28)
    return d
def setup_inputs_low(rng):
    d = setup_inputs(rng)
    s = np.where(np.stack([rng.permutation(T) for r in range(N)]) < 3 * T // 4, 1.0, -1.0)
    d["x"] = tiles(np.exp2(2 * rng.random((N, 128, T, 4))) * s[:, None, :, None] * 2.0 ** 28)
    d["u"] = tiles((1.85 + 2 * rng.random((N, 128, 4, 4))) * 2.0 ** 28)
    d["c"] = tiles((1.9 + 2 * rng.random((N, 128, C, 4)) + 0.1 * rng.random((N, 1, C, 1))) * 2.0 ** 28)
    return d
def setup_inputs_near(rng):
    d = setup_inputs(rng)
    c, x, u = np.zeros((N, 128, C, 4)), np.zeros((N, 128, T, 4)), np.zeros((N, 128, 4, 4))
    same = signed(rng, 64, 4)
    c[:, :64] = signed(rng, N, 64, C, 4)
    c[:, 80:88] = signed(rng, N, 8, C, 4) * 2.0 ** -3
    c[:, 112, :, 0] = 40
    c[:, 120, :, 0] = 0.25
    a, e = int(rng.integers(0, N)), rng.permutation(C)[:M]
    c[a][:64, e] = same[:, None, :]
    u[:, :64, 0] = same
    u[:, 112, 0, 0] = 40
    for r in range(N):
        h = rng.permutation(T) // 4
        i = np.zeros(T)
        i[np.argsort(h, kind="stable")] = np.arange(T) % 4 == 3
        x[r, :64] = signed(rng, 64, T // 4, 4)[:, h]
        x[r, 64:72] = signed(rng, 8, T, 4) * 2.0 ** -11
        x[r, 112, :, 0] = 40
        x[r, 120, :, 0] = (1 + i) * 2.0 ** -11
    d["c"], d["x"], d["u"] = tiles(c * 2.0 ** -4), tiles(x * 2.0 ** -4), tiles(u * 2.0 ** -4)
    return d
def setup_inputs_ties(rng):
    d = setup_inputs(rng)
    c, x, u = np.zeros((N, 128, C, 4)), np.zeros((N, 128, T, 4)), np.zeros((N, 128, 4, 4))
    h = rng.permutation(N * C) // (M // 2 + 3)
    p = signed(rng, 64, int(h.max()) + 1, 4)
    u[:, :64, 0] = p[:, 0]
    for r in range(N):
        c[r, :64] = p[:, h[C * r:C * r + C]]
        g = rng.permutation(T) // 4
        x[r, :64] = signed(rng, 64, T // 4, 4)[:, g]
        x[r, 64:] = signed(rng, 64, T, 4)
    d["c"], d["x"], d["u"] = tiles(c), tiles(x), tiles(u)
    return d
def setup_inputs_spread(rng):
    return {"c": big(wide(rng, N, 128, 4 * C, cols=6)), "x": big(wide(rng, N, 128, 4 * T, cols=6)), "u": wide(rng, N, 128, 16), "w": wide(rng, N, 128, 512 * O)}
def check_inputs(d):
    b = []
    for k, low in (("c", -16), ("x", -16), ("u", -30), ("w", -30)):
        v = np.abs(d[k].astype(np.float32))
        if not (np.isfinite(v).all() and ((v == 0) | (v >= 2.0 ** low) & (v <= 2.0 ** 30)).all()): b.append("a value of " + k)
    return b
def reference(c, x, u, w):
    every = join(*[mx_ref.quantize(np.ascontiguousarray(c[q])) for q in range(N)])
    tok = [mx_ref.quantize(np.ascontiguousarray(x[r])) for r in range(N)]
    s, mark = [], []
    for r in range(N):
        s.append(np.concatenate([mx_ref.matmul(pick(every, np.arange(i, i + 128)), tok[r]) for i in range(0, N * C, 128)]) + np.float32(0))
        a = np.concatenate([u[r], np.zeros((128, 496), BF)], axis=1)
        mark.append(mx_ref.matmul(mx_ref.quantize(a), tok[r])[0] + np.float32(0))
    free, won, made = np.ones(N * C, bool), [], []
    for t in range(R):
        gain = np.zeros(N * C, int)
        for r in range(N): gain = gain + np.sum(s[r] > mark[r], axis=1)
        win = np.argsort(np.where(free, -gain, 1), kind="stable")[:M]
        free[win] = False
        named = [np.argmax(s[r][win] - mark[r], axis=1) for r in range(N)]
        v = decode(pick(every, win))
        for i in range(G):
            v = (v + decode(join(*[pick(tok[(k + i) % N], named[(k + i) % N][k:k + 1]) for k in range(M)]))) * np.float32(0.5)
        q = mx_ref.quantize(np.ascontiguousarray(v.astype(BF)))
        full = pick(q, np.concatenate([np.arange(M), np.full(128 - M, -1)]))
        for r in range(N):
            z = mx_ref.matmul(full, tok[r])[:M] + np.float32(0)
            mark[r] = np.maximum(mark[r], np.max(z, axis=0))
        won.append(win)
        made.append(q)
    q = join(*made)
    n = R * M
    y, oc, osc = np.zeros((N, 128, O * n), np.float32), np.zeros((N, 128, 4 * n), np.uint8), np.zeros((N, 16, n), np.uint8)
    sel, mk = np.zeros((N, 1, n), np.float32), np.zeros((N, 1, T), np.float32)
    for r in range(N):
        for o in range(O): y[r, :, o * n:o * n + n] = mx_ref.matmul(mx_ref.quantize(np.ascontiguousarray(cut(w[r], o))), q)
        oc[r], osc[r] = emit(q)
        sel[r, 0] = np.concatenate(won)
        mk[r, 0] = mark[r]
    return {"y": y, "oc": oc, "osc": osc, "sel": sel, "mk": mk}

@@ -1,0 +1,482 @@
+from concourse.bass import DstId, RemoteDMATransfer
+from concourse.mybir import dt, AluOpType, AxisListType, ActivationFunctionType
+
+N, C, M, R, G = 8, 16, 8, 3, 4
+Q4, U8, BF, F32, I32, U16 = "float8_e4m3fn_x4", "uint8", "bfloat16", "float32", "int32", "uint16"
+
+SCRATCH = {}
+
+
+def _sb(name, cols, dtype):
+    SCRATCH[name] = ("sbuf", [128, cols], dtype)
+
+
+def _mx(name, cols):
+    _sb(name + "q", cols, Q4)
+    _sb(name + "s", cols, U8)
+
+
+for _n, _c in (("ct", 512), ("xt", 512), ("ut", 16), ("wt", 1024), ("hh", 512), ("ind", 512), ("one", 512),
+               ("ee", 2048), ("half", 128), ("ident", 128), ("junk", 128), ("junk2", 128)):
+    _sb(_n, _c, BF)
+for _n, _c in (("zr", 40), ("mult", 40), ("kt", 4), ("aa", 32), ("tiep", 4), ("pen", 4), ("init", 4), ("mcol", 4),
+               ("tt", 128), ("xx", 256), ("yy", 128), ("rk", 4), ("x2", 32), ("y2", 64), ("r1", 4), ("lf", 4),
+               ("m32", 32), ("mb", 128), ("df", 128), ("rm", 128), ("nm", 4), ("row", 48), ("m16", 16), ("pr", 48),
+               ("l3", 4), ("ys", 48)):
+    _sb(_n, _c, F32)
+for _n, _c in (("ip", 1), ("ip32", 1), ("ia", 1), ("ib", 1), ("ic", 1), ("in4", 4), ("in4b", 4), ("im", 16),
+               ("imb", 16), ("ra", 40), ("ra2", 40), ("rb", 40), ("rc", 8), ("ja", 1), ("jb", 1)):
+    _sb(_n, _c, I32)
+for _n, _c in (("rot", 2), ("lst", 4), ("olst", 2), ("off0", 2), ("off1", 2), ("off2", 2)):
+    _sb(_n, _c, U16)
+for _n, _c in (("c0", 128), ("ca", 128), ("hc", 64), ("x", 128), ("w", 256), ("on", 128), ("e", 512), ("mv", 224),
+               ("hi", 128), ("o", 32)):
+    _mx(_n, _c)
+for _t in range(R):
+    _mx("h%d" % _t, 128)
+    _mx("i%d" % _t, 128)
+    _mx("sn%d" % _t, 16)
+    _mx("ht%d" % _t, 16)
+    _mx("tk%d" % _t, 64)
+    _sb("msg%d" % _t, 16, BF)
+    _sb("hg%d" % _t, 8, BF)
+    _sb("land%d" % _t, 160, BF)
+for _n in ("pst", "psa", "pd0", "pd1", "pd2", "pd3", "pz", "pcn"):
+    SCRATCH[_n] = ("psum", [128, 512], F32)
+
+NC, ND = 112, 24
+ARRIVE = ["cc0", "cs0"] + ["%s%d" % (k, t) for t in range(R) for k in ("ga", "tc", "ts")]
+SEMAPHORES = ["sent"] + ARRIVE + ["k%d" % i for i in range(NC)] + ["d%d" % i for i in range(ND)]
+
+A = AluOpType
+ACT = ActivationFunctionType
+X = AxisListType.X
+
+
+def _ways(T, topo, r):
+    me = T.cores[r]
+    others = [(r + d) % N for d in range(1, N)]
+    near = [q for q in others if topo.may_write(me, T.cores[q])]
+    far = [q for q in others if q not in near]
+    hand = [c for c in topo.cores_of(me) if c != me and all(topo.may_write(c, T.cores[q]) for q in far)]
+    hand.sort(key=lambda c: (topo.die(c) != topo.die(me), c))
+    return near, far, hand[:4]
+
+
+def _plan(T, topo, r, kinds):
+    near, far, hand = _ways(T, topo, r)
+    if len(kinds) == 1:
+        return [(kinds[0], [q]) for q in far], [(kinds[0], near)]
+    return [(kinds[h % 2], far[2 * (h // 2):2 * (h // 2) + 2]) for h in range(4)], [(k, near) for k in kinds]
+
+
+def _dst(topo, dst, src):
+    rid, pid = topo.addr(dst, src)
+    return DstId(rid=rid, pnc=pid)
+
+
+def _bits(es):
+    m = 0
+    for e in es:
+        m |= 1 << e
+    return m
+
+
+def _b8(v):
+    return v.bitcast(dt.uint8)
+
+
+def _b32(v):
+    return v.bitcast(dt.uint32)
+
+
+def _views(T, kind, t):
+    if kind == "cc":
+        a, b = _b8(T["c0q"][:, 0:C]), _b8(T["hcq"][:, 0:C])
+        return a, a, b, b
+    if kind == "cs":
+        return T["c0s"][:, 0:C], T["c0s"][:, 0:4 * C], T["hcs"][:, 0:4 * C], T["hcs"][:, 0:C]
+    if kind == "ga":
+        a, b = T["msg%d" % t][:, 0:4], T["hg%d" % t][:, 0:4]
+        return a, a, b, b
+    if kind == "tc":
+        a, b = _b8(T["sn%dq" % t][:, 12:16]), _b8(T["ht%dq" % t][:, 12:16])
+        return a, a, b, b
+    return T["sn%ds" % t][:, 12:16], T["sn%ds" % t][:, 0:16], T["ht%ds" % t][:, 0:16], T["ht%ds" % t][:, 12:16]
+
+
+def _land(T, kind, t, src, dst):
+    d = (src - dst) % N
+    if kind == "cc":
+        return _b8(T["caq"][:, C * src:C * src + C])
+    if kind == "cs":
+        return T["cas"][:, C * src:C * src + C]
+    if kind == "ga":
+        return T["land%d" % t][:, 4 * d:4 * d + 4]
+    if kind == "tc":
+        return _b8(T["tk%dq" % t][:, 12 + 4 * d:16 + 4 * d])
+    return T["tk%ds" % t][:, 12 + 4 * d:16 + 4 * d]
+
+
+def _spread(g, T, topo, core, srcap, kind, t, src, ranks):
+    first = T.cores[ranks[0]]
+    g.remote_dma_fused([RemoteDMATransfer(
+        dst_ids=[_dst(topo, T.cores[q], core) for q in ranks], dma_engine_mask=topo.mask(core, first),
+        remote_sem=T.sem["%s%d" % (kind, t)], src=srcap, dsts=[_land(T, kind, t, src, q) for q in ranks])],
+        local_sem=T.sem["sent"])
+    return len(topo.engines(core, first))
+
+
+STEPS = [(("cc", "cs"), 0)] + [(k, t) for t in range(R) for k in (("ga",), ("tc", "ts"))]
+
+
+def _helper(g, core, T, topo):
+    own = [r for r in range(N) if core in topo.cores_of(T.cores[r])]
+    if not own or core not in _ways(T, topo, own[0])[2]:
+        return
+    r = own[0]
+    h = _ways(T, topo, r)[2].index(core)
+    ne = len(topo.engines(T.cores[r], core)) // 4
+    sent = 0
+    for kinds, t in STEPS:
+        kind, ranks = _plan(T, topo, r, kinds)[0][h]
+        g.wait_ge(T.sem["%s%d" % (kind, t)], ne)
+        sent += _spread(g, T, topo, core, _views(T, kind, t)[3], kind, t, r, ranks)
+    g.wait_ge(T.sem["sent"], sent)
+
+
+def _emit(g, T, ops):
+    eng = {"g": g, "v": g.vector, "s": g.scalar, "t": g.tensor, "y": g.sync}
+    members = {}
+    for i, o in enumerate(ops):
+        if o["grp"] is None:
+            o["grp"] = "#%d" % i
+        members.setdefault(o["grp"], []).append(i)
+    writer, readers = {}, {}
+    known = {q: set() for q in eng}
+    needed = set()
+    for i, o in enumerate(ops):
+        deps = set()
+        for k in o["r"] + o["w"]:
+            if k in writer:
+                deps.add(writer[k])
+        for k in o["w"]:
+            deps.update(readers.get(k, []))
+        kn = known[o["q"]]
+        o["waits"] = []
+        for d in sorted(deps, reverse=True):
+            if d in kn:
+                continue
+            grp = ops[d]["grp"]
+            assert max(members[grp]) < i, (grp, o["r"], o["w"])
+            assert ops[d]["kind"] != "remote"
+            o["waits"].insert(0, grp)
+            needed.add(grp)
+            for m in members[grp]:
+                kn.add(m)
+                kn.update(ops[m]["kn"])
+        o["kn"] = set(kn)
+        for k in o["r"]:
+            if o["fn"] is not None:
+                readers.setdefault(k, []).append(i)
+        for k in o["w"]:
+            writer[k] = i
+            readers[k] = []
+    where = {}
+    free = list(range(NC))
+    last, count = {}, {}
+    nd = [0]
+    for i, o in enumerate(ops):
+        grp = o["grp"]
+        if grp in where or grp not in needed:
+            continue
+        if o["kind"] == "ext":
+            where[grp] = o["ext"]
+        elif o["kind"] == "dma":
+            where[grp] = ("d%d" % nd[0], 16 * len(members[grp]))
+            nd[0] += 1
+        else:
+            s = [k for k in free if all(p in ops[m]["kn"] for p in last.get(k, []) for m in members[grp])][0]
+            free.remove(s)
+            free.append(s)
+            last[s] = members[grp]
+            count[s] = count.get(s, 0) + len(members[grp])
+            where[grp] = ("k%d" % s, count[s])
+    for o in ops:
+        if o["kind"] == "ext":
+            continue
+        e = eng[o["q"]]
+        for grp in o["waits"]:
+            e.wait_ge(T.sem[where[grp][0]], where[grp][1])
+        if o["fn"] is None:
+            continue
+        ins = o["fn"](e)
+        if o["grp"] in needed:
+            ins.then_inc(T.sem[where[o["grp"]][0]], 16 if o["kind"] == "dma" else 1)
+
+
+def rank_program(g, core, T, topo):
+    r = T.rank_of(core)
+    if r is None:
+        _helper(g, core, T, topo)
+        return
+    near, far, hand = _ways(T, topo, r)
+    ops = []
+    sent = [0]
+
+    def op(q, fn, rd, wr, grp=None, kind="c"):
+        ops.append({"q": q, "fn": fn, "r": list(rd), "w": list(wr), "grp": grp, "kind": kind})
+
+    def dma(q, out, in_, rd, wr, grp=None):
+        op(q, lambda e: e.dma_start(out, in_), rd, wr, grp, "dma")
+
+    def arrive(name):
+        n = (N - 1) * len(topo.engines(T.cores[near[0]], core))
+        ops.append({"q": "g", "fn": None, "r": [], "w": [name], "grp": None, "kind": "ext", "ext": (name, n)})
+
+    def send(kinds, t, rd):
+        via, own = _plan(T, topo, r, kinds)
+        es = topo.engines(core, hand[0])
+        k = len(es) // 4
+
+        def fn(e):
+            return e.remote_dma_fused([RemoteDMATransfer(
+                dst_ids=[_dst(topo, hand[j], core)], dma_engine_mask=_bits(es[k * j:k * j + k]),
+                remote_sem=T.sem["%s%d" % (via[j][0], t)], src=_views(T, via[j][0], t)[1],
+                dst=_views(T, via[j][0], t)[2]) for j in range(4)], local_sem=T.sem["sent"])
+        sent[0] += 4 * k
+        op("g", fn, rd, [], None, "remote")
+        for kind, ranks in own:
+            sent[0] += len(topo.engines(core, T.cores[near[0]]))
+            op("g", lambda e, kind=kind, ranks=ranks: _spread(e, T, topo, core, _views(T, kind, t)[0], kind, t, r,
+                                                              ranks), rd, [], None, "remote")
+
+    def memset(ap, v, key, grp=None):
+        op("v", lambda e: e.memset(ap, v), [], [key], grp)
+
+    def quant(name, ap, rd, n=128):
+        op("v", lambda e: e.quantize_mx(T[name + "q"][:, 0:n], T[name + "s"][:, 0:n], ap), rd, [name])
+
+    def mm(out, w, wa, x, xa, rd):
+        op("t", lambda e: e.matmul_mx(T[out][:, 0:128], T[w + "q"][:, wa:wa + 128], T[w + "s"][:, wa:wa + 128],
+                                      T[x + "q"][:, xa:xa + 128], T[x + "s"][:, xa:xa + 128], True, True), rd, [out])
+
+    def ts(out, in0, s1, s2, o0, o1, rd, wr, grp=None):
+        if o1 is None:
+            op("v", lambda e: e.tensor_scalar(out, in0, s1, None, o0), rd, wr, grp)
+        else:
+            op("v", lambda e: e.tensor_scalar(out, in0, s1, s2, o0, o1), rd, wr, grp)
+
+    def tt(out, a, b, o, rd, wr, grp=None):
+        op("v", lambda e: e.tensor_tensor(out, a, b, o), rd, wr, grp)
+
+    def cp(out, a, rd, wr, grp=None):
+        op("v", lambda e: e.tensor_copy(out, a), rd, wr, grp)
+
+    def tr(out, a, rd, wr, grp=None):
+        op("v", lambda e: e.transpose(out, a), rd, wr, grp)
+
+    def iota(out, pattern, base, cm, key, flt=False, grp=None):
+        if flt:
+            op("g", lambda e: e.iota(out, pattern, base, cm, allow_small_or_imprecise_dtypes=True), [], [key], grp)
+        else:
+            op("g", lambda e: e.iota(out, pattern, base, cm), [], [key], grp)
+
+    def pickq(dst, a, n, src, wa, wb, off, rd, wr):
+        op("v", lambda e: e.tensor_copy(_b32(T[dst + "q"][:, a:a + n]), _b32(T[src + "q"][:, wa:wb]).indirect(off)),
+           rd, wr)
+
+    def picks(dst, a, n, src, wa, wb, off, rd, wr):
+        op("s", lambda e: e.activation(T[dst + "s"][:, a:a + n], T[src + "s"][:, wa:wb].indirect(off), ACT.Copy),
+           rd, wr)
+
+    def rank_of(col, c, key):
+        op("s", lambda e: e.activation(T["junk"][:], T["yy"][:], ACT.Sign, bias=T["xx"][:, 64 * c + 63:64 * c + 64],
+                                       scale=-1.0, accum_out=col),
+           ["yy0", "yy1", "yy2", "yy3", "xx%d" % c], [key, "junk"])
+
+    dma("y", T["ct"][:, 0:4 * C], T.c[:], [], ["ct_a"])
+    dma("y", T["xt"][:], T.x[:], [], ["xt"])
+    dma("s", T["ut"][:], T.u[:], [], ["ut"])
+    memset(T["ct"][:, 4 * C:512], 0.0, "ct_b")
+    memset(T["hh"][:], 0.0, "hh_z", "fill")
+    memset(T["ind"][:], 0.0, "ind", "fill")
+    memset(T["one"][:], 1.0, "one", "fill")
+    memset(T["half"][:], 0.5, "half", "fill")
+    quant("c0", T["ct"][:], ["ct_a", "ct_b"])
+    send(("cc", "cs"), 0, ["c0"])
+    dma("y", _b8(T["caq"][:, C * r:C * r + C]), _b8(T["c0q"][:, 0:C]), ["c0"], ["ca_q"], "own")
+    dma("y", T["cas"][:, C * r:C * r + C], T["c0s"][:, 0:C], ["c0"], ["ca_s"], "own")
+
+    iota(T["ip"][:], [[0, 1]], 0, 1, "ip", grp="io1")
+    iota(T["ip32"][:], [[0, 1]], 0, 32, "ip32", grp="io1")
+    iota(T["in4"][:], [[32, 4]], 0, 1, "in4", grp="io1")
+    op("g", lambda e: e.affine_select(T["ident"][:], T["half"][:], [[-1, 128]], A.is_equal, 0.0, 0, 1),
+       ["half"], ["ident"])
+    iota(T["aa"][:], [[0, 4], [-512, 8]], 127 * 256, 1, "aa_z", True, "io2")
+    iota(T["im"][:], [[1, 16]], 128, -1, "im", grp="io2")
+    iota(T["ra"][:], [[4, 8], [4, 5]], 28 - 4 * r, 0, "ra", grp="io2")
+    iota(T["rb"][:], [[0, 8], [1, 5]], 11, 0, "rb", grp="io2")
+    iota(T["rc"][:], [[1, 8]], 48, 0, "rc", grp="io2")
+
+    quant("x", T["xt"][:], ["xt"])
+    cp(T["hh"][:, 16:20], T["ut"][:, 0:4], ["ut", "hh_z"], ["hh_u"])
+    quant("on", T["one"][:], ["one"])
+    quant("hi", T["hh"][:], ["hh_z", "hh_u"])
+    mm("pz", "x", 0, "hi", 0, ["x", "hi"])
+    memset(T["zr"][:], 0.0, "zr", "fill2")
+    for t in range(R):
+        memset(T["land%d" % t][:, 32:160], 0.0, "lz%d" % t, "fill2")
+    for s, v in enumerate((0.0, 1.0, 0.5, 0.5, 0.5)):
+        memset(T["mult"][:, s:40:5], v, "mult%d" % s, "fill2")
+    for i in range(G):
+        memset(T["kt"][:, i:i + 1], float(256 * (127 - 2 * ((r - i) % M))), "kt%d" % i, "fill2")
+    memset(T["row"][:, 40:48], 0.0, "row_z", "fill2")
+    op("v", lambda e: e.tensor_reduce(T["mcol"][:, 0:1], T["pz"][:, 4:5], X, A.max), ["pz"], ["m0"])
+    ts(T["ia"][:], T["ip"][:], 96, None, A.bitwise_and, None, ["ip"], ["ia"])
+    ts(T["in4b"][:], T["in4"][:], 127, None, A.bitwise_and, None, ["in4"], ["in4b"])
+    tt(T["ib"][:], T["ia"][:], T["ip32"][:], A.add, ["ia", "ip32"], ["ib"])
+    ts(T["tiep"][:], T["in4b"][:], -1.0 / 128, 127.0 / 128, A.mult, A.add, ["in4b"], ["tiep"])
+    ts(T["ic"][:], T["ib"][:], 127, None, A.bitwise_and, None, ["ib"], ["ic"])
+    cp(T["rot"][:, 0:1], T["ic"][:], ["ic"], ["rot"])
+    for b in range(4):
+        for k in range(4):
+            op("s", lambda e, b=b, k=k: e.activation(T["ee"][:, 512 * b + k:512 * b + 512:4], T["ident"][:], ACT.Copy,
+                                                     scale=1.0 if k == b else 0.0),
+               ["ident"], ["ee%d" % (4 * b + k)], "ee")
+    op("t", None, ["on", "ca_q", "ca_s"], [])
+    op("v", None, ["m0", "rot", "tiep", "zr"], [])
+
+    arrive("cc0")
+    arrive("cs0")
+    mm("pst", "x", 0, "ca", 0, ["x", "ca_q", "ca_s", "cc0", "cs0"])
+    mm("psa", "ca", 0, "x", 0, ["x", "ca_q", "ca_s", "cc0", "cs0"])
+
+    hkeys = ["hh_z", "hh_u"]
+    for t in range(R):
+        m = T["mcol"][:, t:t + 1]
+        mk_, msg, off = "m%d" % t, T["msg%d" % t], T["off%d" % t][:, 0:1]
+        ts(T["ind"][:, 0:512:4], T["pst"][:, 0:128], m, None, A.is_gt, None, ["pst", mk_], ["ind"])
+        quant("i%d" % t, T["ind"][:], ["ind"])
+        mm("pcn", "on", 0, "i%d" % t, 0, ["on", "i%d" % t])
+        tr(T["tt"][:], T["pcn"][:, 0:128], ["pcn"], ["tt"])
+        cp(msg[:], T["tt"][:].indirect(T["rot"][:, 0:1]), ["tt", "rot"], ["msg%d" % t])
+        send(("ga",), t, ["msg%d" % t])
+        ts(T["m32"][:], T["zr"][:, 0:32], m, None, A.add, None, ["zr", mk_], ["m32"])
+        tt(T["init"][:], msg[:, 0:4], T["tiep"][:], A.add, ["msg%d" % t, "tiep"], ["init"])
+        for b in range(4):
+            tr(T["mb"][0:32, 32 * b:32 * b + 32], T["m32"][32 * b:32 * b + 32, :], ["m32"], ["mb%d" % b], "mb%d" % t)
+        cp(T["mb"][32:64, :], T["mb"][0:32, :], ["mb0", "mb1", "mb2", "mb3"], ["mbb"])
+        cp(T["mb"][64:128, :], T["mb"][0:64, :], ["mb0", "mb1", "mb2", "mb3", "mbb"], ["mbc"])
+        tt(T["df"][:], T["psa"][:, 0:128], T["mb"][:], A.subtract,
+           ["psa", "mb0", "mb1", "mb2", "mb3", "mbb", "mbc"], ["df"])
+        op("v", lambda e: e.tensor_tensor_scan(T["rm"][:], T["df"][:], T["df"][:], T["df"][:, 0:1], A.max, A.max),
+           ["df"], ["rm"])
+        op("s", lambda e, t=t: e.activation(T["junk2"][:], T["rm"][:], ACT.Sign, bias=T["rm"][:, 127:128], scale=-1.0,
+                                            accum_out=T["nm"][:, t:t + 1]), ["rm"], ["nm%d" % t, "junk2"])
+        if t == 0:
+            ts(T["imb"][:], T["im"][:], 15, None, A.bitwise_and, None, ["im"], ["imb"])
+            ts(T["ra2"][:], T["ra"][:], 31, None, A.bitwise_and, None, ["ra"], ["ra2"])
+        for j in range(2):
+            ts(T["aa"][:, 16 * j + 12:16 * j + 16], T["kt"][:], T["nm"][:, t:t + 1], None, A.add, None,
+               ["kt0", "nm%d" % t, "aa_z"], ["aa%d" % j], "aa%d" % t)
+        if t == 0:
+            dma("y", _b8(T["mvq"][:, 48:128]), _b8(T["xq"][:, 0:80]), ["x", "rm"], ["mv_fq"], "mvf")
+            dma("y", T["mvs"][:, 48:128], T["xs"][:, 0:80], ["x", "rm"], ["mv_fs"], "mvf")
+            dma("y", T["wt"][:], T.w[:], ["rm"], ["wt"])
+        op("v", None, ["aa0", "aa1", "init", "lz%d" % t], [])
+        arrive("ga%d" % t)
+        land = T["land%d" % t]
+        for c in range(4):
+            op("v", lambda e, c=c, land=land: e.tensor_tensor_scan(
+                T["xx"][:, 64 * c + 26:64 * c + 64], land[:, 4 + c:156:4], T["zr"][:, 0:38], T["init"][:, c:c + 1],
+                A.add, A.add), ["ga%d" % t, "lz%d" % t, "zr", "init"], ["xx%d" % c])
+        for c in range(4):
+            tr(T["yy"][:, 32 * c:32 * c + 32], T["xx"][:, 64 * c + 32:64 * c + 64], ["xx%d" % c], ["yy%d" % c],
+               "yy%d" % t)
+        rank_of(T["rk"][:, 0:1], 0, "rk0")
+        ts(T["x2"][:], T["aa"][:], 1.0 / 256, T["rk"][:, 0:1], A.mult, A.subtract, ["aa_z", "aa0", "aa1", "rk0"], ["x2"])
+        tr(T["y2"][0:64, 0:32], T["x2"][0:64, :], ["x2"], ["y2a"], "y2%d" % t)
+        tr(T["y2"][0:64, 32:64], T["x2"][64:128, :], ["x2"], ["y2b"], "y2%d" % t)
+        op("v", lambda e, t=t: e.tensor_reduce(T["r1"][0:64, t:t + 1], T["y2"][0:64, :], X, A.min,
+                                               apply_absolute_value=True), ["y2a", "y2b"], ["r1%d" % t])
+        for a in range(4):
+            ts(T["off%d" % t][32 * a:32 * a + 32, 0:1], T["r1"][0:32, t:t + 1], T["r1"][32:64, t:t + 1], 256.0,
+               A.min, A.mult, ["r1%d" % t], ["off%d_%d" % (t, a)], "off%d" % t)
+        offk = ["off%d_%d" % (t, a) for a in range(4)]
+        sn, tk = "sn%d" % t, "tk%d" % t
+        pickq(sn, 0, 16, "x", 0, 128, off, offk + ["x"], [sn + "q"])
+        picks(sn, 0, 16, "x", 0, 128, off, offk + ["x"], [sn + "s"])
+        send(("tc", "ts"), t, [sn + "q", sn + "s"])
+        pickq(tk, 0, 16, "x", 0, 128, off, offk + ["x"], [tk + "q0"])
+        picks(tk, 0, 16, "x", 0, 128, off, offk + ["x"], [tk + "s0"])
+        pickq(tk, 48, 16, "ca", 0, 128, off, offk + ["ca_q", "cc0"], [tk + "q1"])
+        picks(tk, 48, 16, "ca", 0, 128, off, offk + ["ca_s", "cs0"], [tk + "s1"])
+        ts(T["lf"][0:32, t:t + 1], T["r1"][0:32, t:t + 1], T["r1"][32:64, t:t + 1], 256.0, A.min, A.mult,
+           ["r1%d" % t], ["lf%d" % t])
+        if t == 0:
+            ts(T["m16"][:], T["imb"][:], 0.0, None, A.is_equal, None, ["imb"], ["m16"])
+            tt(T["row"][:, 0:40], T["ra2"][:], T["rb"][:], A.add, ["ra2", "rb"], ["row"])
+            quant("e", T["ee"][:], ["ee%d" % k for k in range(16)], 512)
+            cp(T["row"][:, 0:40:5], T["rc"][:], ["rc"], ["row"])
+            for c in range(3):
+                tt(T["pr"][:, 16 * c:16 * c + 16], T["row"][:, 16 * c:16 * c + 16], T["m16"][:], A.mult,
+                   ["row", "row_z", "m16"], ["pr%d" % c], "pr")
+            for c in range(3):
+                op("v", lambda e, c=c: e.tensor_reduce(T["l3"][:, c:c + 1], T["pr"][:, 16 * c:16 * c + 16], X, A.add),
+                   ["pr%d" % c], ["l3%d" % c], "l3")
+            cp(T["lst"][:, 0:3], T["l3"][:, 0:3], ["l30", "l31", "l32"], ["lst"])
+        if t < R - 1:
+            for c in range(1, 4):
+                rank_of(T["rk"][:, c:c + 1], c, "rk%d" % c)
+            ts(T["pen"][:], T["rk"][:], 112.0, -2048.0, A.is_gt, A.mult, ["rk0", "rk1", "rk2", "rk3"], ["pen"])
+            tt(T["tiep"][:], T["tiep"][:], T["pen"][:], A.add, ["pen", "tiep"], ["tiep"])
+        dma("y", T.sel[0:1, M * t:M * t + M], T["lf"][0:M, t:t + 1], ["lf%d" % t, tk + "q1"], ["o_sel%d" % t])
+        if t == 1:
+            quant("w", T["wt"][:], ["wt"], 256)
+            ts(T["ja"][:], T["ip"][:], 15, None, A.bitwise_and, None, ["ip"], ["ja"])
+            ts(T["olst"][:, 0:1], T["ja"][:], 5.0, 9.0, A.mult, A.add, ["ja"], ["ol0"])
+            ts(T["jb"][:], T["ja"][:], 7.0, 5.0, A.min, A.mult, ["ja"], ["jb"])
+            ts(T["olst"][:, 1:2], T["jb"][:], 89.0, None, A.add, None, ["jb"], ["ol1"])
+        late = ["ol0", "ol1", "w"] if t == R - 1 else []
+        op("v", None, ["lst", tk + "q0", tk + "q1", "tiep"] + late, [])
+        op("s", None, ["lst", tk + "s0", tk + "s1"] + late[:2], [])
+        op("t", None, ["mv_fq", "e"] + late[2:], [])
+        arrive("tc%d" % t)
+        arrive("ts%d" % t)
+        pa = (0, 128, 176)[t]
+        va = (0, 48, 96)[t]
+        pickq("mv", pa, 48, tk, 0, 64, T["lst"][:, 0:3], ["lst", tk + "q0", tk + "q1", "tc%d" % t], ["mvq%d" % t])
+        picks("mv", pa, 48, tk, 0, 64, T["lst"][:, 0:3], ["lst", tk + "s0", tk + "s1", "ts%d" % t], ["mvs%d" % t])
+        mvk = ["mv_fq", "mv_fs", "e", "mvq%d" % t, "mvs%d" % t] + (["mvq1", "mvs1"] if t == 2 else [])
+        for b in range(4):
+            mm("pd%d" % b, "e", 128 * b, "mv", va, mvk)
+        h0 = 4 * (5 + 40 * t)
+        for b in range(4):
+            op("v", lambda e, b=b, h0=h0, k=pa - va: e.tensor_tensor_scan(
+                T["hh"][:, h0 + b:h0 + 160:4], T["mult"][:], T["pd%d" % b][:, k:k + 40], 0.0, A.mult, A.add),
+               ["pd%d" % b, "mult0", "hh_z", "hi" if t == 0 else "h%d" % (t - 1)], ["hh%d_%d" % (t, b)], "hv%d" % t)
+            hkeys.append("hh%d_%d" % (t, b))
+        quant("h%d" % t, T["hh"][:], hkeys)
+        mm("pz", "x", 0, "h%d" % t, 0, ["x", "h%d" % t])
+        if t == R - 1:
+            mm("pcn", "w", 0, "h2", 0, ["w", "h2"])
+            mm("psa", "w", 128, "h2", 0, ["w", "h2"])
+            pickq("o", 0, 32, "h2", 0, 128, T["olst"][:, 0:2], ["ol0", "ol1", "h2"], ["oq"])
+            picks("o", 0, 32, "h2", 0, 128, T["olst"][:, 0:2], ["ol0", "ol1", "h2"], ["os"])
+        op("v", lambda e, t=t: e.tensor_reduce(T["mcol"][:, t + 1:t + 2], T["pz"][:, 4:5 + 40 * (t + 1):5], X, A.max),
+           ["pz"], ["m%d" % (t + 1)])
+
+    n = R * M
+    cp(T["ys"][:, 0:n], T["pcn"][:, 9:125:5], ["pcn"], ["ys0"])
+    op("y", None, ["o_sel0", "o_sel1", "o_sel2"], [])
+    dma("y", T.oc[:, 0:4 * n], _b8(T["oq"][:, 0:n]), ["oq"], ["o_oc"], "outy")
+    for k in range(4):
+        dma("y" if k < 2 else "s", T.osc[4 * k:4 * k + 4, 0:n], T["os"][32 * k:32 * k + 4, 0:n], ["os"],
+            ["o_os%d" % k], "outy")
+    dma("y", T.mk[0:1, :], T["mcol"][:, R:R + 1], ["m%d" % R], ["o_mk"], "outy")
+    op("s", lambda e: e.activation(T["ys"][:, n:2 * n], T["psa"][:, 9:125:5], ACT.Copy), ["psa"], ["ys1"])
+    dma("s", T.y[:], T["ys"][:], ["ys0", "ys1"], ["o_y"], "outy")
+    op("g", lambda e: e.wait_ge(T.sem["sent"], sent[0]), [], [], None, "remote")
+    op("y", None, ["o_oc"], [])
+    _emit(g, T, ops)

@@ -17,20 +17,20 @@ def _mx(name, cols):
 
 
 for _n, _c in (("ct", 512), ("xt", 512), ("ut", 16), ("wt", 1024), ("hh", 512), ("ind", 512), ("one", 512),
-               ("ee", 2048), ("half", 128), ("ident", 128), ("junk", 128), ("junk2", 128)):
+               ("ee", 2048), ("half", 128), ("ident", 128), ("junk", 128)):
     _sb(_n, _c, BF)
-for _n, _c in (("zr", 40), ("mult", 40), ("kt", 4), ("aa", 32), ("tiep", 4), ("pen", 4), ("init", 4), ("mcol", 4),
-               ("tt", 128), ("xx", 256), ("yy", 128), ("rk", 4), ("x2", 32), ("y2", 64), ("r1", 4), ("lf", 4),
-               ("m32", 32), ("mb", 128), ("df", 128), ("rm", 128), ("nm", 4), ("row", 48), ("m16", 16), ("pr", 48),
-               ("l3", 4), ("ys", 48)):
+for _n, _c in (("zr", 40), ("mult", 40), ("kt", 4), ("aa", 32), ("ab", 32), ("tiep", 2), ("pen", 2), ("init", 2),
+               ("mcol", 4), ("idf", 2), ("xx", 128), ("yy", 128), ("rk", 2), ("x2", 32), ("y2", 64), ("r1", 4),
+               ("lf", 4), ("m32", 32), ("mb", 128), ("df", 128), ("rm", 128), ("nm", 4), ("row", 48), ("m48", 48),
+               ("pr", 48), ("l3", 4), ("ys", 48)):
     _sb(_n, _c, F32)
-for _n, _c in (("ip", 1), ("ip32", 1), ("ia", 1), ("ib", 1), ("ic", 1), ("in4", 4), ("in4b", 4), ("im", 16),
-               ("imb", 16), ("ra", 40), ("ra2", 40), ("rb", 40), ("rc", 8), ("ja", 1), ("jb", 1)):
+for _n, _c in (("ip", 1), ("ip4", 1), ("ia", 1), ("ib", 1), ("pa", 8), ("pb", 8), ("im", 48), ("imb", 48),
+               ("ra", 40), ("ra2", 40), ("rb", 40), ("rc", 8), ("ja", 1), ("jb", 1)):
     _sb(_n, _c, I32)
-for _n, _c in (("rot", 2), ("lst", 4), ("olst", 2), ("off0", 2), ("off1", 2), ("off2", 2)):
+for _n, _c in (("l16", 2), ("pl", 8), ("lst", 4), ("olst", 2), ("off0", 2), ("off1", 2), ("off2", 2)):
     _sb(_n, _c, U16)
-for _n, _c in (("c0", 128), ("ca", 128), ("hc", 64), ("x", 128), ("w", 256), ("on", 128), ("e", 512), ("mv", 224),
-               ("hi", 128), ("o", 32)):
+for _n, _c in (("c0", 128), ("ca", 128), ("cb", 128), ("hc", 64), ("x", 128), ("w", 256), ("on", 128), ("e", 512),
+               ("mv", 272), ("hi", 128), ("o", 32)):
     _mx(_n, _c)
 for _t in range(R):
     _mx("h%d" % _t, 128)
@@ -38,15 +38,16 @@ for _t in range(R):
     _mx("sn%d" % _t, 16)
     _mx("ht%d" % _t, 16)
     _mx("tk%d" % _t, 64)
-    _sb("msg%d" % _t, 16, BF)
-    _sb("hg%d" % _t, 8, BF)
-    _sb("land%d" % _t, 160, BF)
+    _sb("msg%d" % _t, 32, F32)
+    _sb("hg%d" % _t, 4, F32)
+    _sb("land%d" % _t, 80, F32)
 for _n in ("pst", "psa", "pd0", "pd1", "pd2", "pd3", "pz", "pcn"):
     SCRATCH[_n] = ("psum", [128, 512], F32)
 
-NC, ND = 112, 24
+NC, ND = 122, 10
 ARRIVE = ["cc0", "cs0"] + ["%s%d" % (k, t) for t in range(R) for k in ("ga", "tc", "ts")]
-SEMAPHORES = ["sent"] + ARRIVE + ["k%d" % i for i in range(NC)] + ["d%d" % i for i in range(ND)]
+LOCAL = ["sent", "sent0", "sentl"]
+SEMAPHORES = LOCAL + ARRIVE + ["k%d" % i for i in range(NC)] + ["d%d" % i for i in range(ND)]
 
 A = AluOpType
 ACT = ActivationFunctionType
@@ -65,9 +66,15 @@ def _ways(T, topo, r):
 
 def _plan(T, topo, r, kinds):
     near, far, hand = _ways(T, topo, r)
-    if len(kinds) == 1:
-        return [(kinds[0], [q]) for q in far], [(kinds[0], near)]
-    return [(kinds[h % 2], far[2 * (h // 2):2 * (h // 2) + 2]) for h in range(4)], [(k, near) for k in kinds]
+    me = T.cores[r]
+    es = topo.engines(me, hand[0])
+    if kinds[0] == "cc":
+        es = [e for e in es if e not in topo.engines(me, T.cores[near[0]])]
+    step = len(kinds)
+    k = len(es) // step
+    feeds = [(kind, es[k * j:k * j + k], [(hand[j], far[0:2]), (hand[j + step], far[2:4])])
+             for j, kind in enumerate(kinds)]
+    return feeds, [(kind, near) for kind in kinds]
 
 
 def _dst(topo, dst, src):
@@ -97,7 +104,7 @@ def _views(T, kind, t):
     if kind == "cs":
         return T["c0s"][:, 0:C], T["c0s"][:, 0:4 * C], T["hcs"][:, 0:4 * C], T["hcs"][:, 0:C]
     if kind == "ga":
-        a, b = T["msg%d" % t][:, 0:4], T["hg%d" % t][:, 0:4]
+        a, b = T["msg%d" % t][:, 0:2], T["hg%d" % t][:, 0:2]
         return a, a, b, b
     if kind == "tc":
         a, b = _b8(T["sn%dq" % t][:, 12:16]), _b8(T["ht%dq" % t][:, 12:16])
@@ -112,18 +119,18 @@ def _land(T, kind, t, src, dst):
     if kind == "cs":
         return T["cas"][:, C * src:C * src + C]
     if kind == "ga":
-        return T["land%d" % t][:, 4 * d:4 * d + 4]
+        return T["land%d" % t][:, 2 * d:2 * d + 2]
     if kind == "tc":
         return _b8(T["tk%dq" % t][:, 12 + 4 * d:16 + 4 * d])
     return T["tk%ds" % t][:, 12 + 4 * d:16 + 4 * d]
 
 
-def _spread(g, T, topo, core, srcap, kind, t, src, ranks):
+def _spread(g, T, topo, core, srcap, kind, t, src, ranks, local):
     first = T.cores[ranks[0]]
     g.remote_dma_fused([RemoteDMATransfer(
         dst_ids=[_dst(topo, T.cores[q], core) for q in ranks], dma_engine_mask=topo.mask(core, first),
         remote_sem=T.sem["%s%d" % (kind, t)], src=srcap, dsts=[_land(T, kind, t, src, q) for q in ranks])],
-        local_sem=T.sem["sent"])
+        local_sem=T.sem[local])
     return len(topo.engines(core, first))
 
 
@@ -132,17 +139,18 @@ STEPS = [(("cc", "cs"), 0)] + [(k, t) for t in range(R) for k in (("ga",), ("tc"
 
 def _helper(g, core, T, topo):
     own = [r for r in range(N) if core in topo.cores_of(T.cores[r])]
-    if not own or core not in _ways(T, topo, own[0])[2]:
+    if not own:
         return
     r = own[0]
-    h = _ways(T, topo, r)[2].index(core)
-    ne = len(topo.engines(T.cores[r], core)) // 4
     sent = 0
     for kinds, t in STEPS:
-        kind, ranks = _plan(T, topo, r, kinds)[0][h]
-        g.wait_ge(T.sem["%s%d" % (kind, t)], ne)
-        sent += _spread(g, T, topo, core, _views(T, kind, t)[3], kind, t, r, ranks)
-    g.wait_ge(T.sem["sent"], sent)
+        for kind, es, dsts in _plan(T, topo, r, kinds)[0]:
+            for c, ranks in dsts:
+                if c == core:
+                    g.wait_ge(T.sem["%s%d" % (kind, t)], len(es))
+                    sent += _spread(g, T, topo, core, _views(T, kind, t)[3], kind, t, r, ranks, "sent")
+    if sent:
+        g.wait_ge(T.sem["sent"], sent)
 
 
 def _emit(g, T, ops):
@@ -162,7 +170,7 @@ def _emit(g, T, ops):
                 deps.add(writer[k])
         for k in o["w"]:
             deps.update(readers.get(k, []))
-        kn = known[o["q"]]
+        kn = known[o["q"]] if o["kind"] != "ext" else set()
         o["waits"] = []
         for d in sorted(deps, reverse=True):
             if d in kn:
@@ -221,8 +229,9 @@ def rank_program(g, core, T, topo):
         _helper(g, core, T, topo)
         return
     near, far, hand = _ways(T, topo, r)
+    nout = len(topo.engines(core, T.cores[near[0]]))
     ops = []
-    sent = [0]
+    sent = {k: 0 for k in LOCAL}
 
     def op(q, fn, rd, wr, grp=None, kind="c"):
         ops.append({"q": q, "fn": fn, "r": list(rd), "w": list(wr), "grp": grp, "kind": kind})
@@ -230,32 +239,31 @@ def rank_program(g, core, T, topo):
     def dma(q, out, in_, rd, wr, grp=None):
         op(q, lambda e: e.dma_start(out, in_), rd, wr, grp, "dma")
 
-    def arrive(name):
-        n = (N - 1) * len(topo.engines(T.cores[near[0]], core))
+    def arrive(name, n=(N - 1) * nout):
         ops.append({"q": "g", "fn": None, "r": [], "w": [name], "grp": None, "kind": "ext", "ext": (name, n)})
 
-    def send(kinds, t, rd):
-        via, own = _plan(T, topo, r, kinds)
-        es = topo.engines(core, hand[0])
-        k = len(es) // 4
+    def send(kinds, t, rd, local="sent"):
+        feeds, own = _plan(T, topo, r, kinds)
 
         def fn(e):
             return e.remote_dma_fused([RemoteDMATransfer(
-                dst_ids=[_dst(topo, hand[j], core)], dma_engine_mask=_bits(es[k * j:k * j + k]),
-                remote_sem=T.sem["%s%d" % (via[j][0], t)], src=_views(T, via[j][0], t)[1],
-                dst=_views(T, via[j][0], t)[2]) for j in range(4)], local_sem=T.sem["sent"])
-        sent[0] += 4 * k
+                dst_ids=[_dst(topo, c, core) for c, _ in dsts], dma_engine_mask=_bits(es),
+                remote_sem=T.sem["%s%d" % (kind, t)], src=_views(T, kind, t)[1],
+                dsts=[_views(T, kind, t)[2] for _ in dsts]) for kind, es, dsts in feeds], local_sem=T.sem[local])
+        sent[local] += sum(len(es) for _, es, _ in feeds)
         op("g", fn, rd, [], None, "remote")
         for kind, ranks in own:
-            sent[0] += len(topo.engines(core, T.cores[near[0]]))
+            sent[local] += nout
             op("g", lambda e, kind=kind, ranks=ranks: _spread(e, T, topo, core, _views(T, kind, t)[0], kind, t, r,
-                                                              ranks), rd, [], None, "remote")
+                                                              ranks, local), rd, [], None, "remote")
+        if local != "sent":
+            arrive(local, sent[local])
 
     def memset(ap, v, key, grp=None):
         op("v", lambda e: e.memset(ap, v), [], [key], grp)
 
-    def quant(name, ap, rd, n=128):
-        op("v", lambda e: e.quantize_mx(T[name + "q"][:, 0:n], T[name + "s"][:, 0:n], ap), rd, [name])
+    def quant(name, ap, rd, n=128, a=0, key=None):
+        op("v", lambda e: e.quantize_mx(T[name + "q"][:, a:a + n], T[name + "s"][:, a:a + n], ap), rd, [key or name])
 
     def mm(out, w, wa, x, xa, rd):
         op("t", lambda e: e.matmul_mx(T[out][:, 0:128], T[w + "q"][:, wa:wa + 128], T[w + "s"][:, wa:wa + 128],
@@ -290,111 +298,125 @@ def rank_program(g, core, T, topo):
         op("s", lambda e: e.activation(T[dst + "s"][:, a:a + n], T[src + "s"][:, wa:wb].indirect(off), ACT.Copy),
            rd, wr)
 
-    def rank_of(col, c, key):
-        op("s", lambda e: e.activation(T["junk"][:], T["yy"][:], ACT.Sign, bias=T["xx"][:, 64 * c + 63:64 * c + 64],
-                                       scale=-1.0, accum_out=col),
-           ["yy0", "yy1", "yy2", "yy3", "xx%d" % c], [key, "junk"])
+    def rank_of(c):
+        op("s", lambda e: e.activation(T["junk"][:], T["yy"][:], ACT.Sign, bias=T["xx"][:, 63 + c:64 + c],
+                                       scale=-1.0, accum_out=T["rk"][:, c:c + 1]),
+           ["yy0", "yy1", "yy2", "xx%d" % c], ["rk%d" % c, "junk"])
 
     dma("y", T["ct"][:, 0:4 * C], T.c[:], [], ["ct_a"])
     dma("y", T["xt"][:], T.x[:], [], ["xt"])
     dma("s", T["ut"][:], T.u[:], [], ["ut"])
+    memset(T["half"][:], 0.5, "half")
     memset(T["ct"][:, 4 * C:512], 0.0, "ct_b")
-    memset(T["hh"][:], 0.0, "hh_z", "fill")
-    memset(T["ind"][:], 0.0, "ind", "fill")
-    memset(T["one"][:], 1.0, "one", "fill")
-    memset(T["half"][:], 0.5, "half", "fill")
-    quant("c0", T["ct"][:], ["ct_a", "ct_b"])
-    send(("cc", "cs"), 0, ["c0"])
-    dma("y", _b8(T["caq"][:, C * r:C * r + C]), _b8(T["c0q"][:, 0:C]), ["c0"], ["ca_q"], "own")
-    dma("y", T["cas"][:, C * r:C * r + C], T["c0s"][:, 0:C], ["c0"], ["ca_s"], "own")
-
-    iota(T["ip"][:], [[0, 1]], 0, 1, "ip", grp="io1")
-    iota(T["ip32"][:], [[0, 1]], 0, 32, "ip32", grp="io1")
-    iota(T["in4"][:], [[32, 4]], 0, 1, "in4", grp="io1")
+    memset(T["hh"][:], 0.0, "hh_z")
+    iota(T["ip"][:], [[0, 1]], 0, 1, "ip")
     op("g", lambda e: e.affine_select(T["ident"][:], T["half"][:], [[-1, 128]], A.is_equal, 0.0, 0, 1),
        ["half"], ["ident"])
-    iota(T["aa"][:], [[0, 4], [-512, 8]], 127 * 256, 1, "aa_z", True, "io2")
-    iota(T["im"][:], [[1, 16]], 128, -1, "im", grp="io2")
+    op("v", None, ["ct_b", "hh_z"], [])
+    quant("c0", T["ct"][:], ["ct_a", "ct_b"])
+    send(("cc", "cs"), 0, ["c0"], "sent0")
+    dma("y", T["wt"][:], T.w[:], ["sent0"], ["wt"])
+
+    iota(T["ip4"][:], [[0, 1]], 0, 4, "ip4", grp="io1")
+    iota(T["pa"][:], [[1, 4], [0, 2]], 0, 4, "pa", grp="io1")
+    iota(T["ab"][:], [[0, 4], [-512, 8]], 127 * 256, 0, "ab", True, "io1")
+    iota(T["zr"][:], [[0, 40]], 0, 0, "zr", True, "io1")
+    iota(T["im"][:], [[1, 48]], 128, -1, "im", grp="io2")
     iota(T["ra"][:], [[4, 8], [4, 5]], 28 - 4 * r, 0, "ra", grp="io2")
     iota(T["rb"][:], [[0, 8], [1, 5]], 11, 0, "rb", grp="io2")
     iota(T["rc"][:], [[1, 8]], 48, 0, "rc", grp="io2")
+    cut = min(G, r + 1)
+    iota(T["kt"][:, 0:cut], [[512, cut]], 256 * (127 - 2 * r), 0, "kt0", True, "io3")
+    if cut < G:
+        iota(T["kt"][:, cut:G], [[512, G - cut]], 256 * (127 - 2 * (M - 1)), 0, "kt1", True, "io3")
+    iota(T["land0"][:, 16:80], [[0, 64]], 0, 0, "lz0", True, "io3")
 
+    ts(T["ja"][:], T["ip"][:], 15, None, A.bitwise_and, None, ["ip"], ["ja"])
+    memset(T["one"][:], 0.0, "one")
+    cp(T["l16"][:, 0:1], T["ja"][:], ["ja"], ["l16"])
     quant("x", T["xt"][:], ["xt"])
     cp(T["hh"][:, 16:20], T["ut"][:, 0:4], ["ut", "hh_z"], ["hh_u"])
-    quant("on", T["one"][:], ["one"])
+    op("v", lambda e: e.memset(T["one"][:, 0:512:129], 1.0), ["one"], ["one0"], "fill1")
+    op("v", lambda e: e.memset(T["one"][:, 7:512:127], 1.0), ["one"], ["one1"], "fill1")
+    pickq("ca", C * r, C, "c0", 0, C, T["l16"][:, 0:1], ["l16", "c0"], ["ca_q"])
+    picks("ca", C * r, C, "c0", 0, C, T["l16"][:, 0:1], ["l16", "c0"], ["ca_s"])
     quant("hi", T["hh"][:], ["hh_z", "hh_u"])
     mm("pz", "x", 0, "hi", 0, ["x", "hi"])
-    memset(T["zr"][:], 0.0, "zr", "fill2")
-    for t in range(R):
-        memset(T["land%d" % t][:, 32:160], 0.0, "lz%d" % t, "fill2")
-    for s, v in enumerate((0.0, 1.0, 0.5, 0.5, 0.5)):
-        memset(T["mult"][:, s:40:5], v, "mult%d" % s, "fill2")
-    for i in range(G):
-        memset(T["kt"][:, i:i + 1], float(256 * (127 - 2 * ((r - i) % M))), "kt%d" % i, "fill2")
+    quant("on", T["one"][:], ["one", "one0", "one1"])
+    memset(T["ind"][:, 128:512], 0.0, "ind_z", "fill2")
     memset(T["row"][:, 40:48], 0.0, "row_z", "fill2")
     op("v", lambda e: e.tensor_reduce(T["mcol"][:, 0:1], T["pz"][:, 4:5], X, A.max), ["pz"], ["m0"])
-    ts(T["ia"][:], T["ip"][:], 96, None, A.bitwise_and, None, ["ip"], ["ia"])
-    ts(T["in4b"][:], T["in4"][:], 127, None, A.bitwise_and, None, ["in4"], ["in4b"])
-    tt(T["ib"][:], T["ia"][:], T["ip32"][:], A.add, ["ia", "ip32"], ["ib"])
-    ts(T["tiep"][:], T["in4b"][:], -1.0 / 128, 127.0 / 128, A.mult, A.add, ["in4b"], ["tiep"])
-    ts(T["ic"][:], T["ib"][:], 127, None, A.bitwise_and, None, ["ib"], ["ic"])
-    cp(T["rot"][:, 0:1], T["ic"][:], ["ic"], ["rot"])
+    ts(T["ia"][:], T["ip"][:], 5, None, A.logical_shift_right, None, ["ip"], ["ia"], "c1")
+    ts(T["ib"][:], T["ip4"][:], 127, None, A.bitwise_and, None, ["ip4"], ["ib"], "c1")
+    ts(T["pb"][:], T["pa"][:], 63, None, A.bitwise_and, None, ["pa"], ["pb"], "c1")
+    tt(T["idf"][:, 0:1], T["ib"][:], T["ia"][:], A.add, ["ia", "ib"], ["idf0"], "c2")
+    tt(T["idf"][:, 1:2], T["ib"][:], T["ia"][:], A.subtract, ["ia", "ib"], ["idf1"], "c2")
+    ts(T["pl"][:, 0:8:2], T["pb"][:, 0:8:2], 0.0, None, A.add, None, ["pb"], ["pl0"], "c2")
+    ts(T["pl"][:, 1:8:2], T["pb"][:, 1:8:2], 64.0, None, A.add, None, ["pb"], ["pl1"], "c2")
+    ts(T["tiep"][:, 0:1], T["idf"][:, 0:1], -1.0 / 128, 127.0 / 128, A.mult, A.add, ["idf0"], ["tiep"], "c3")
+    ts(T["tiep"][:, 1:2], T["idf"][:, 1:2], -1.0 / 128, 124.0 / 128, A.mult, A.add, ["idf1"], ["tiep1"], "c3")
+    ts(T["aa"][:], T["ab"][:], T["idf"][:, 0:1], None, A.add, None, ["ab", "idf0"], ["aa_z"], "c3")
+    ts(T["imb"][:], T["im"][:], 15, None, A.bitwise_and, None, ["im"], ["imb"], "c4")
+    ts(T["ra2"][:], T["ra"][:], 31, None, A.bitwise_and, None, ["ra"], ["ra2"], "c4")
+    ts(T["m48"][:], T["imb"][:], 0.0, None, A.is_equal, None, ["imb"], ["m48"], "c5")
+    tt(T["row"][:, 0:40], T["ra2"][:], T["rb"][:], A.add, ["ra2", "rb"], ["row"], "c5")
     for b in range(4):
         for k in range(4):
             op("s", lambda e, b=b, k=k: e.activation(T["ee"][:, 512 * b + k:512 * b + 512:4], T["ident"][:], ACT.Copy,
                                                      scale=1.0 if k == b else 0.0),
                ["ident"], ["ee%d" % (4 * b + k)], "ee")
     op("t", None, ["on", "ca_q", "ca_s"], [])
-    op("v", None, ["m0", "rot", "tiep", "zr"], [])
+    op("v", None, ["m0", "tiep", "zr", "row", "pl0", "ind_z"], [])
 
     arrive("cc0")
     arrive("cs0")
     mm("pst", "x", 0, "ca", 0, ["x", "ca_q", "ca_s", "cc0", "cs0"])
-    mm("psa", "ca", 0, "x", 0, ["x", "ca_q", "ca_s", "cc0", "cs0"])
 
     hkeys = ["hh_z", "hh_u"]
+    mbk = ["mb0", "mb1", "mb2", "mb3"]
     for t in range(R):
         m = T["mcol"][:, t:t + 1]
         mk_, msg, off = "m%d" % t, T["msg%d" % t], T["off%d" % t][:, 0:1]
-        ts(T["ind"][:, 0:512:4], T["pst"][:, 0:128], m, None, A.is_gt, None, ["pst", mk_], ["ind"])
-        quant("i%d" % t, T["ind"][:], ["ind"])
+        op("s", lambda e, m=m: e.activation(T["m32"][:], T["zr"][:, 0:32], ACT.Identity, bias=m), ["zr", mk_], ["m32"])
+        ts(T["ind"][:, 0:128], T["pst"][:, 0:128], m, None, A.is_gt, None, ["pst", mk_], ["ind"])
+        quant("i%d" % t, T["ind"][:], ["ind", "ind_z"])
         mm("pcn", "on", 0, "i%d" % t, 0, ["on", "i%d" % t])
-        tr(T["tt"][:], T["pcn"][:, 0:128], ["pcn"], ["tt"])
-        cp(msg[:], T["tt"][:].indirect(T["rot"][:, 0:1]), ["tt", "rot"], ["msg%d" % t])
-        send(("ga",), t, ["msg%d" % t])
-        ts(T["m32"][:], T["zr"][:, 0:32], m, None, A.add, None, ["zr", mk_], ["m32"])
-        tt(T["init"][:], msg[:, 0:4], T["tiep"][:], A.add, ["msg%d" % t, "tiep"], ["init"])
         for b in range(4):
+            if b == 2:
+                tr(msg[:], T["pcn"][:, 0:32], ["pcn"], ["msg%d" % t])
+                send(("ga",), t, ["msg%d" % t])
             tr(T["mb"][0:32, 32 * b:32 * b + 32], T["m32"][32 * b:32 * b + 32, :], ["m32"], ["mb%d" % b], "mb%d" % t)
-        cp(T["mb"][32:64, :], T["mb"][0:32, :], ["mb0", "mb1", "mb2", "mb3"], ["mbb"])
-        cp(T["mb"][64:128, :], T["mb"][0:64, :], ["mb0", "mb1", "mb2", "mb3", "mbb"], ["mbc"])
-        tt(T["df"][:], T["psa"][:, 0:128], T["mb"][:], A.subtract,
-           ["psa", "mb0", "mb1", "mb2", "mb3", "mbb", "mbc"], ["df"])
+        if t == 0:
+            pickq("cb", 0, 128, "ca", 0, 128, T["pl"][:, 0:8], ["pl0", "pl1", "ca_q", "cc0"], ["cbq"])
+            picks("cb", 0, 128, "ca", 0, 128, T["pl"][:, 0:8], ["pl0", "pl1", "ca_s", "cs0"], ["cbs"])
+            mm("psa", "cb", 0, "x", 0, ["x", "cbq", "cbs"])
+        tt(T["init"][:], msg[:, 0:2], T["tiep"][:], A.add, ["msg%d" % t, "tiep", "tiep1"], ["init"])
+        op("s", lambda e: e.activation(T["mb"][64:96, :], T["mb"][0:32, :], ACT.Copy), mbk, ["mbc"], "mc%d" % t)
+        cp(T["mb"][32:64, :], T["mb"][0:32, :], mbk, ["mbb"], "mc%d" % t)
+        cp(T["mb"][96:128, :], T["mb"][0:32, :], mbk, ["mbd"], "mc%d" % t)
+        tt(T["df"][:], T["psa"][:, 0:128], T["mb"][:], A.subtract, ["psa", "mbb", "mbc", "mbd"] + mbk, ["df"])
         op("v", lambda e: e.tensor_tensor_scan(T["rm"][:], T["df"][:], T["df"][:], T["df"][:, 0:1], A.max, A.max),
            ["df"], ["rm"])
-        op("s", lambda e, t=t: e.activation(T["junk2"][:], T["rm"][:], ACT.Sign, bias=T["rm"][:, 127:128], scale=-1.0,
-                                            accum_out=T["nm"][:, t:t + 1]), ["rm"], ["nm%d" % t, "junk2"])
+        op("s", lambda e, t=t: e.activation(T["junk"][:], T["rm"][:], ACT.Sign, bias=T["rm"][:, 127:128], scale=-1.0,
+                                            accum_out=T["nm"][:, t:t + 1]), ["rm"], ["nm%d" % t, "junk"])
         if t == 0:
-            ts(T["imb"][:], T["im"][:], 15, None, A.bitwise_and, None, ["im"], ["imb"])
-            ts(T["ra2"][:], T["ra"][:], 31, None, A.bitwise_and, None, ["ra"], ["ra2"])
+            quant("e", T["ee"][:], ["ee%d" % k for k in range(16)], 512)
+        op("v", None, ["init", "lz%d" % t, "rm", "kt0"], [])
+        op("s", None, ["nm%d" % t], [])
+        arrive("ga%d" % t)
+        land = T["land%d" % t]
+        for c, out in enumerate((T["xx"][:, 26:64], T["xx"][:, 101:63:-1])):
+            op("v", lambda e, c=c, land=land, out=out: e.tensor_tensor_scan(
+                out, land[:, 2 + c:78:2], T["zr"][:, 0:38], T["init"][:, c:c + 1],
+                A.add, A.add), ["ga%d" % t, "lz%d" % t, "zr", "init"], ["xx%d" % c], "xx%d" % t)
+        tr(T["yy"][:, 0:64], T["xx"][:, 32:96], ["xx0", "xx1"], ["yy0"], "yy%d" % t)
+        tr(T["yy"][0:64, 64:128], T["xx"][64:128, 32:96], ["xx0", "xx1"], ["yy1"], "yy%d" % t)
+        tr(T["yy"][64:128, 64:128], T["xx"][0:64, 32:96], ["xx0", "xx1"], ["yy2"], "yy%d" % t)
+        rank_of(0)
         for j in range(2):
             ts(T["aa"][:, 16 * j + 12:16 * j + 16], T["kt"][:], T["nm"][:, t:t + 1], None, A.add, None,
                ["kt0", "nm%d" % t, "aa_z"], ["aa%d" % j], "aa%d" % t)
-        if t == 0:
-            dma("y", _b8(T["mvq"][:, 48:128]), _b8(T["xq"][:, 0:80]), ["x", "rm"], ["mv_fq"], "mvf")
-            dma("y", T["mvs"][:, 48:128], T["xs"][:, 0:80], ["x", "rm"], ["mv_fs"], "mvf")
-            dma("y", T["wt"][:], T.w[:], ["rm"], ["wt"])
-        op("v", None, ["aa0", "aa1", "init", "lz%d" % t], [])
-        arrive("ga%d" % t)
-        land = T["land%d" % t]
-        for c in range(4):
-            op("v", lambda e, c=c, land=land: e.tensor_tensor_scan(
-                T["xx"][:, 64 * c + 26:64 * c + 64], land[:, 4 + c:156:4], T["zr"][:, 0:38], T["init"][:, c:c + 1],
-                A.add, A.add), ["ga%d" % t, "lz%d" % t, "zr", "init"], ["xx%d" % c])
-        for c in range(4):
-            tr(T["yy"][:, 32 * c:32 * c + 32], T["xx"][:, 64 * c + 32:64 * c + 64], ["xx%d" % c], ["yy%d" % c],
-               "yy%d" % t)
-        rank_of(T["rk"][:, 0:1], 0, "rk0")
+        op("v", None, ["aa0"], [])
         ts(T["x2"][:], T["aa"][:], 1.0 / 256, T["rk"][:, 0:1], A.mult, A.subtract, ["aa_z", "aa0", "aa1", "rk0"], ["x2"])
         tr(T["y2"][0:64, 0:32], T["x2"][0:64, :], ["x2"], ["y2a"], "y2%d" % t)
         tr(T["y2"][0:64, 32:64], T["x2"][64:128, :], ["x2"], ["y2b"], "y2%d" % t)
@@ -407,55 +429,62 @@ def rank_program(g, core, T, topo):
         sn, tk = "sn%d" % t, "tk%d" % t
         pickq(sn, 0, 16, "x", 0, 128, off, offk + ["x"], [sn + "q"])
         picks(sn, 0, 16, "x", 0, 128, off, offk + ["x"], [sn + "s"])
-        send(("tc", "ts"), t, [sn + "q", sn + "s"])
+        send(("tc", "ts"), t, [sn + "q", sn + "s"], "sentl" if t == R - 1 else "sent")
+        if t < R - 1:
+            rank_of(1)
+            iota(T["land%d" % (t + 1)][:, 16:80], [[0, 64]], 0, 0, "lz%d" % (t + 1), True)
         pickq(tk, 0, 16, "x", 0, 128, off, offk + ["x"], [tk + "q0"])
         picks(tk, 0, 16, "x", 0, 128, off, offk + ["x"], [tk + "s0"])
         pickq(tk, 48, 16, "ca", 0, 128, off, offk + ["ca_q", "cc0"], [tk + "q1"])
         picks(tk, 48, 16, "ca", 0, 128, off, offk + ["ca_s", "cs0"], [tk + "s1"])
+        if t == 0:
+            cp(T["row"][:, 0:40:5], T["rc"][:], ["rc"], ["row"])
+            memset(T["mult"][:], 0.5, "mult")
         ts(T["lf"][0:32, t:t + 1], T["r1"][0:32, t:t + 1], T["r1"][32:64, t:t + 1], 256.0, A.min, A.mult,
            ["r1%d" % t], ["lf%d" % t])
         if t == 0:
-            ts(T["m16"][:], T["imb"][:], 0.0, None, A.is_equal, None, ["imb"], ["m16"])
-            tt(T["row"][:, 0:40], T["ra2"][:], T["rb"][:], A.add, ["ra2", "rb"], ["row"])
-            quant("e", T["ee"][:], ["ee%d" % k for k in range(16)], 512)
-            cp(T["row"][:, 0:40:5], T["rc"][:], ["rc"], ["row"])
-            for c in range(3):
-                tt(T["pr"][:, 16 * c:16 * c + 16], T["row"][:, 16 * c:16 * c + 16], T["m16"][:], A.mult,
-                   ["row", "row_z", "m16"], ["pr%d" % c], "pr")
+            tt(T["pr"][:], T["row"][:], T["m48"][:], A.mult, ["row", "row_z", "m48"], ["pr"])
+            op("v", lambda e: e.memset(T["mult"][:, 0:40:5], 0.0), ["mult"], ["mult0"], "mu")
+            op("v", lambda e: e.memset(T["mult"][:, 1:40:5], 1.0), ["mult"], ["mult1"], "mu")
             for c in range(3):
                 op("v", lambda e, c=c: e.tensor_reduce(T["l3"][:, c:c + 1], T["pr"][:, 16 * c:16 * c + 16], X, A.add),
-                   ["pr%d" % c], ["l3%d" % c], "l3")
-            cp(T["lst"][:, 0:3], T["l3"][:, 0:3], ["l30", "l31", "l32"], ["lst"])
+                   ["pr"], ["l3%d" % c], "l3")
         if t < R - 1:
-            for c in range(1, 4):
-                rank_of(T["rk"][:, c:c + 1], c, "rk%d" % c)
-            ts(T["pen"][:], T["rk"][:], 112.0, -2048.0, A.is_gt, A.mult, ["rk0", "rk1", "rk2", "rk3"], ["pen"])
-            tt(T["tiep"][:], T["tiep"][:], T["pen"][:], A.add, ["pen", "tiep"], ["tiep"])
-        dma("y", T.sel[0:1, M * t:M * t + M], T["lf"][0:M, t:t + 1], ["lf%d" % t, tk + "q1"], ["o_sel%d" % t])
+            ts(T["pen"][:], T["rk"][:], 112.0, -2048.0, A.is_gt, A.mult, ["rk0", "rk1"], ["pen"])
+        if t == 0:
+            cp(T["lst"][:, 0:3], T["l3"][:, 0:3], ["l30", "l31", "l32"], ["lst"])
+            quant("mv", T["xt"][:], ["xt"], 128, 48, "mvf")
         if t == 1:
-            quant("w", T["wt"][:], ["wt"], 256)
-            ts(T["ja"][:], T["ip"][:], 15, None, A.bitwise_and, None, ["ip"], ["ja"])
-            ts(T["olst"][:, 0:1], T["ja"][:], 5.0, 9.0, A.mult, A.add, ["ja"], ["ol0"])
             ts(T["jb"][:], T["ja"][:], 7.0, 5.0, A.min, A.mult, ["ja"], ["jb"])
+            ts(T["olst"][:, 0:1], T["ja"][:], 5.0, 9.0, A.mult, A.add, ["ja"], ["ol0"])
+        if t < R - 1:
+            tt(T["tiep"][:], T["tiep"][:], T["pen"][:], A.add, ["pen", "tiep", "tiep1"], ["tiep"])
+        if t == 1:
             ts(T["olst"][:, 1:2], T["jb"][:], 89.0, None, A.add, None, ["jb"], ["ol1"])
+        if t == R - 1:
+            quant("w", T["wt"][:], ["wt"], 256)
+            for k in range(R):
+                dma("y", T.sel[0:1, M * k:M * k + M], T["lf"][0:M, k:k + 1], ["lf%d" % k, "sentl"], ["o_sel%d" % k],
+                    "osel")
         late = ["ol0", "ol1", "w"] if t == R - 1 else []
-        op("v", None, ["lst", tk + "q0", tk + "q1", "tiep"] + late, [])
+        op("v", None, ["lst", tk + "q0", tk + "q1", "tiep", "mult0", "mvf"] + late, [])
         op("s", None, ["lst", tk + "s0", tk + "s1"] + late[:2], [])
-        op("t", None, ["mv_fq", "e"] + late[2:], [])
+        op("t", None, ["mvf", "e"] + late[2:], [])
         arrive("tc%d" % t)
         arrive("ts%d" % t)
-        pa = (0, 128, 176)[t]
-        va = (0, 48, 96)[t]
+        pa = (0, 176, 224)[t]
+        va = (0, 96, 144)[t]
         pickq("mv", pa, 48, tk, 0, 64, T["lst"][:, 0:3], ["lst", tk + "q0", tk + "q1", "tc%d" % t], ["mvq%d" % t])
         picks("mv", pa, 48, tk, 0, 64, T["lst"][:, 0:3], ["lst", tk + "s0", tk + "s1", "ts%d" % t], ["mvs%d" % t])
-        mvk = ["mv_fq", "mv_fs", "e", "mvq%d" % t, "mvs%d" % t] + (["mvq1", "mvs1"] if t == 2 else [])
+        mvk = ["mvf", "e", "mvq%d" % t, "mvs%d" % t] + (["mvq1", "mvs1"] if t == 2 else [])
         for b in range(4):
             mm("pd%d" % b, "e", 128 * b, "mv", va, mvk)
         h0 = 4 * (5 + 40 * t)
         for b in range(4):
             op("v", lambda e, b=b, h0=h0, k=pa - va: e.tensor_tensor_scan(
                 T["hh"][:, h0 + b:h0 + 160:4], T["mult"][:], T["pd%d" % b][:, k:k + 40], 0.0, A.mult, A.add),
-               ["pd%d" % b, "mult0", "hh_z", "hi" if t == 0 else "h%d" % (t - 1)], ["hh%d_%d" % (t, b)], "hv%d" % t)
+               ["pd%d" % b, "mult0", "mult1", "hh_z", "hi" if t == 0 else "h%d" % (t - 1)], ["hh%d_%d" % (t, b)],
+               "hv%d" % t)
             hkeys.append("hh%d_%d" % (t, b))
         quant("h%d" % t, T["hh"][:], hkeys)
         mm("pz", "x", 0, "h%d" % t, 0, ["x", "h%d" % t])
@@ -469,14 +498,13 @@ def rank_program(g, core, T, topo):
 
     n = R * M
     cp(T["ys"][:, 0:n], T["pcn"][:, 9:125:5], ["pcn"], ["ys0"])
-    op("y", None, ["o_sel0", "o_sel1", "o_sel2"], [])
+    cp(T["ys"][:, n:2 * n], T["psa"][:, 9:125:5], ["psa"], ["ys1"])
     dma("y", T.oc[:, 0:4 * n], _b8(T["oq"][:, 0:n]), ["oq"], ["o_oc"], "outy")
     for k in range(4):
         dma("y" if k < 2 else "s", T.osc[4 * k:4 * k + 4, 0:n], T["os"][32 * k:32 * k + 4, 0:n], ["os"],
             ["o_os%d" % k], "outy")
     dma("y", T.mk[0:1, :], T["mcol"][:, R:R + 1], ["m%d" % R], ["o_mk"], "outy")
-    op("s", lambda e: e.activation(T["ys"][:, n:2 * n], T["psa"][:, 9:125:5], ACT.Copy), ["psa"], ["ys1"])
     dma("s", T.y[:], T["ys"][:], ["ys0", "ys1"], ["o_y"], "outy")
-    op("g", lambda e: e.wait_ge(T.sem["sent"], sent[0]), [], [], None, "remote")
-    op("y", None, ["o_oc"], [])
+    op("g", lambda e: e.wait_ge(T.sem["sent"], sent["sent"]), [], [], None, "remote")
+    op("y", None, ["o_sel0", "o_oc"], [])
     _emit(g, T, ops)

from concourse.bass import DstId, RemoteDMATransfer
from concourse.mybir import dt, AluOpType, AxisListType, ActivationFunctionType

N, C, M, R, G = 8, 16, 8, 3, 4
Q4, U8, BF, F32, I32, U16 = "float8_e4m3fn_x4", "uint8", "bfloat16", "float32", "int32", "uint16"

SCRATCH = {}


def _sb(name, cols, dtype):
    SCRATCH[name] = ("sbuf", [128, cols], dtype)


def _mx(name, cols):
    _sb(name + "q", cols, Q4)
    _sb(name + "s", cols, U8)


for _n, _c in (("ct", 512), ("xt", 512), ("ut", 16), ("wt", 1024), ("hh", 512), ("ind", 512), ("one", 512),
               ("ee", 2048), ("half", 128), ("ident", 128), ("junk", 128)):
    _sb(_n, _c, BF)
for _n, _c in (("zr", 40), ("mult", 40), ("kt", 4), ("aa", 32), ("ab", 32), ("tiep", 2), ("pen", 2), ("init", 2),
               ("mcol", 4), ("idf", 2), ("xx", 128), ("yy", 128), ("rk", 2), ("x2", 32), ("y2", 64), ("r1", 4),
               ("lf", 4), ("m32", 32), ("mb", 128), ("df", 128), ("rm", 128), ("nm", 4), ("row", 48), ("m48", 48),
               ("pr", 48), ("l3", 4), ("ys", 48)):
    _sb(_n, _c, F32)
for _n, _c in (("ip", 1), ("ip4", 1), ("ia", 1), ("ib", 1), ("pa", 8), ("pb", 8), ("im", 48), ("imb", 48),
               ("ra", 40), ("ra2", 40), ("rb", 40), ("rc", 8), ("ja", 1), ("jb", 1)):
    _sb(_n, _c, I32)
for _n, _c in (("l16", 2), ("pl", 8), ("lst", 4), ("olst", 2), ("off0", 2), ("off1", 2), ("off2", 2)):
    _sb(_n, _c, U16)
for _n, _c in (("c0", 128), ("ca", 128), ("cb", 128), ("hc", 64), ("x", 128), ("w", 256), ("on", 128), ("e", 512),
               ("mv", 272), ("hi", 128), ("o", 32)):
    _mx(_n, _c)
for _t in range(R):
    _mx("h%d" % _t, 128)
    _mx("i%d" % _t, 128)
    _mx("sn%d" % _t, 16)
    _mx("ht%d" % _t, 16)
    _mx("tk%d" % _t, 64)
    _sb("msg%d" % _t, 32, F32)
    _sb("hg%d" % _t, 4, F32)
    _sb("land%d" % _t, 80, F32)
for _n in ("pst", "psa", "pd0", "pd1", "pd2", "pd3", "pz", "pcn"):
    SCRATCH[_n] = ("psum", [128, 512], F32)

NC, ND = 122, 10
ARRIVE = ["cc0", "cs0"] + ["%s%d" % (k, t) for t in range(R) for k in ("ga", "tc", "ts")]
LOCAL = ["sent", "sent0", "sentl"]
SEMAPHORES = LOCAL + ARRIVE + ["k%d" % i for i in range(NC)] + ["d%d" % i for i in range(ND)]

A = AluOpType
ACT = ActivationFunctionType
X = AxisListType.X


def _ways(T, topo, r):
    me = T.cores[r]
    others = [(r + d) % N for d in range(1, N)]
    near = [q for q in others if topo.may_write(me, T.cores[q])]
    far = [q for q in others if q not in near]
    hand = [c for c in topo.cores_of(me) if c != me and all(topo.may_write(c, T.cores[q]) for q in far)]
    hand.sort(key=lambda c: (topo.die(c) != topo.die(me), c))
    return near, far, hand[:4]


def _plan(T, topo, r, kinds):
    near, far, hand = _ways(T, topo, r)
    me = T.cores[r]
    es = topo.engines(me, hand[0])
    if kinds[0] == "cc":
        es = [e for e in es if e not in topo.engines(me, T.cores[near[0]])]
    step = len(kinds)
    k = len(es) // step
    feeds = [(kind, es[k * j:k * j + k], [(hand[j], far[0:2]), (hand[j + step], far[2:4])])
             for j, kind in enumerate(kinds)]
    return feeds, [(kind, near) for kind in kinds]


def _dst(topo, dst, src):
    rid, pid = topo.addr(dst, src)
    return DstId(rid=rid, pnc=pid)


def _bits(es):
    m = 0
    for e in es:
        m |= 1 << e
    return m


def _b8(v):
    return v.bitcast(dt.uint8)


def _b32(v):
    return v.bitcast(dt.uint32)


def _views(T, kind, t):
    if kind == "cc":
        a, b = _b8(T["c0q"][:, 0:C]), _b8(T["hcq"][:, 0:C])
        return a, a, b, b
    if kind == "cs":
        return T["c0s"][:, 0:C], T["c0s"][:, 0:4 * C], T["hcs"][:, 0:4 * C], T["hcs"][:, 0:C]
    if kind == "ga":
        a, b = T["msg%d" % t][:, 0:2], T["hg%d" % t][:, 0:2]
        return a, a, b, b
    if kind == "tc":
        a, b = _b8(T["sn%dq" % t][:, 12:16]), _b8(T["ht%dq" % t][:, 12:16])
        return a, a, b, b
    return T["sn%ds" % t][:, 12:16], T["sn%ds" % t][:, 0:16], T["ht%ds" % t][:, 0:16], T["ht%ds" % t][:, 12:16]


def _land(T, kind, t, src, dst):
    d = (src - dst) % N
    if kind == "cc":
        return _b8(T["caq"][:, C * src:C * src + C])
    if kind == "cs":
        return T["cas"][:, C * src:C * src + C]
    if kind == "ga":
        return T["land%d" % t][:, 2 * d:2 * d + 2]
    if kind == "tc":
        return _b8(T["tk%dq" % t][:, 12 + 4 * d:16 + 4 * d])
    return T["tk%ds" % t][:, 12 + 4 * d:16 + 4 * d]


def _spread(g, T, topo, core, srcap, kind, t, src, ranks, local):
    first = T.cores[ranks[0]]
    g.remote_dma_fused([RemoteDMATransfer(
        dst_ids=[_dst(topo, T.cores[q], core) for q in ranks], dma_engine_mask=topo.mask(core, first),
        remote_sem=T.sem["%s%d" % (kind, t)], src=srcap, dsts=[_land(T, kind, t, src, q) for q in ranks])],
        local_sem=T.sem[local])
    return len(topo.engines(core, first))


STEPS = [(("cc", "cs"), 0)] + [(k, t) for t in range(R) for k in (("ga",), ("tc", "ts"))]


def _helper(g, core, T, topo):
    own = [r for r in range(N) if core in topo.cores_of(T.cores[r])]
    if not own:
        return
    r = own[0]
    sent = 0
    for kinds, t in STEPS:
        for kind, es, dsts in _plan(T, topo, r, kinds)[0]:
            for c, ranks in dsts:
                if c == core:
                    g.wait_ge(T.sem["%s%d" % (kind, t)], len(es))
                    sent += _spread(g, T, topo, core, _views(T, kind, t)[3], kind, t, r, ranks, "sent")
    if sent:
        g.wait_ge(T.sem["sent"], sent)


def _emit(g, T, ops):
    eng = {"g": g, "v": g.vector, "s": g.scalar, "t": g.tensor, "y": g.sync}
    members = {}
    for i, o in enumerate(ops):
        if o["grp"] is None:
            o["grp"] = "#%d" % i
        members.setdefault(o["grp"], []).append(i)
    writer, readers = {}, {}
    known = {q: set() for q in eng}
    needed = set()
    for i, o in enumerate(ops):
        deps = set()
        for k in o["r"] + o["w"]:
            if k in writer:
                deps.add(writer[k])
        for k in o["w"]:
            deps.update(readers.get(k, []))
        kn = known[o["q"]] if o["kind"] != "ext" else set()
        o["waits"] = []
        for d in sorted(deps, reverse=True):
            if d in kn:
                continue
            grp = ops[d]["grp"]
            assert max(members[grp]) < i, (grp, o["r"], o["w"])
            assert ops[d]["kind"] != "remote"
            o["waits"].insert(0, grp)
            needed.add(grp)
            for m in members[grp]:
                kn.add(m)
                kn.update(ops[m]["kn"])
        o["kn"] = set(kn)
        for k in o["r"]:
            if o["fn"] is not None:
                readers.setdefault(k, []).append(i)
        for k in o["w"]:
            writer[k] = i
            readers[k] = []
    where = {}
    free = list(range(NC))
    last, count = {}, {}
    nd = [0]
    for i, o in enumerate(ops):
        grp = o["grp"]
        if grp in where or grp not in needed:
            continue
        if o["kind"] == "ext":
            where[grp] = o["ext"]
        elif o["kind"] == "dma":
            where[grp] = ("d%d" % nd[0], 16 * len(members[grp]))
            nd[0] += 1
        else:
            s = [k for k in free if all(p in ops[m]["kn"] for p in last.get(k, []) for m in members[grp])][0]
            free.remove(s)
            free.append(s)
            last[s] = members[grp]
            count[s] = count.get(s, 0) + len(members[grp])
            where[grp] = ("k%d" % s, count[s])
    for o in ops:
        if o["kind"] == "ext":
            continue
        e = eng[o["q"]]
        for grp in o["waits"]:
            e.wait_ge(T.sem[where[grp][0]], where[grp][1])
        if o["fn"] is None:
            continue
        ins = o["fn"](e)
        if o["grp"] in needed:
            ins.then_inc(T.sem[where[o["grp"]][0]], 16 if o["kind"] == "dma" else 1)


def rank_program(g, core, T, topo):
    r = T.rank_of(core)
    if r is None:
        _helper(g, core, T, topo)
        return
    near, far, hand = _ways(T, topo, r)
    nout = len(topo.engines(core, T.cores[near[0]]))
    ops = []
    sent = {k: 0 for k in LOCAL}

    def op(q, fn, rd, wr, grp=None, kind="c"):
        ops.append({"q": q, "fn": fn, "r": list(rd), "w": list(wr), "grp": grp, "kind": kind})

    def dma(q, out, in_, rd, wr, grp=None):
        op(q, lambda e: e.dma_start(out, in_), rd, wr, grp, "dma")

    def arrive(name, n=(N - 1) * nout):
        ops.append({"q": "g", "fn": None, "r": [], "w": [name], "grp": None, "kind": "ext", "ext": (name, n)})

    def send(kinds, t, rd, local="sent"):
        feeds, own = _plan(T, topo, r, kinds)

        def fn(e):
            return e.remote_dma_fused([RemoteDMATransfer(
                dst_ids=[_dst(topo, c, core) for c, _ in dsts], dma_engine_mask=_bits(es),
                remote_sem=T.sem["%s%d" % (kind, t)], src=_views(T, kind, t)[1],
                dsts=[_views(T, kind, t)[2] for _ in dsts]) for kind, es, dsts in feeds], local_sem=T.sem[local])
        sent[local] += sum(len(es) for _, es, _ in feeds)
        op("g", fn, rd, [], None, "remote")
        for kind, ranks in own:
            sent[local] += nout
            op("g", lambda e, kind=kind, ranks=ranks: _spread(e, T, topo, core, _views(T, kind, t)[0], kind, t, r,
                                                              ranks, local), rd, [], None, "remote")
        if local != "sent":
            arrive(local, sent[local])

    def memset(ap, v, key, grp=None):
        op("v", lambda e: e.memset(ap, v), [], [key], grp)

    def quant(name, ap, rd, n=128, a=0, key=None):
        op("v", lambda e: e.quantize_mx(T[name + "q"][:, a:a + n], T[name + "s"][:, a:a + n], ap), rd, [key or name])

    def mm(out, w, wa, x, xa, rd):
        op("t", lambda e: e.matmul_mx(T[out][:, 0:128], T[w + "q"][:, wa:wa + 128], T[w + "s"][:, wa:wa + 128],
                                      T[x + "q"][:, xa:xa + 128], T[x + "s"][:, xa:xa + 128], True, True), rd, [out])

    def ts(out, in0, s1, s2, o0, o1, rd, wr, grp=None):
        if o1 is None:
            op("v", lambda e: e.tensor_scalar(out, in0, s1, None, o0), rd, wr, grp)
        else:
            op("v", lambda e: e.tensor_scalar(out, in0, s1, s2, o0, o1), rd, wr, grp)

    def tt(out, a, b, o, rd, wr, grp=None):
        op("v", lambda e: e.tensor_tensor(out, a, b, o), rd, wr, grp)

    def cp(out, a, rd, wr, grp=None):
        op("v", lambda e: e.tensor_copy(out, a), rd, wr, grp)

    def tr(out, a, rd, wr, grp=None):
        op("v", lambda e: e.transpose(out, a), rd, wr, grp)

    def iota(out, pattern, base, cm, key, flt=False, grp=None):
        if flt:
            op("g", lambda e: e.iota(out, pattern, base, cm, allow_small_or_imprecise_dtypes=True), [], [key], grp)
        else:
            op("g", lambda e: e.iota(out, pattern, base, cm), [], [key], grp)

    def pickq(dst, a, n, src, wa, wb, off, rd, wr):
        op("v", lambda e: e.tensor_copy(_b32(T[dst + "q"][:, a:a + n]), _b32(T[src + "q"][:, wa:wb]).indirect(off)),
           rd, wr)

    def picks(dst, a, n, src, wa, wb, off, rd, wr):
        op("s", lambda e: e.activation(T[dst + "s"][:, a:a + n], T[src + "s"][:, wa:wb].indirect(off), ACT.Copy),
           rd, wr)

    def rank_of(c):
        op("s", lambda e: e.activation(T["junk"][:], T["yy"][:], ACT.Sign, bias=T["xx"][:, 63 + c:64 + c],
                                       scale=-1.0, accum_out=T["rk"][:, c:c + 1]),
           ["yy0", "yy1", "yy2", "xx%d" % c], ["rk%d" % c, "junk"])

    dma("y", T["ct"][:, 0:4 * C], T.c[:], [], ["ct_a"])
    dma("y", T["xt"][:], T.x[:], [], ["xt"])
    dma("s", T["ut"][:], T.u[:], [], ["ut"])
    memset(T["half"][:], 0.5, "half")
    memset(T["ct"][:, 4 * C:512], 0.0, "ct_b")
    memset(T["hh"][:], 0.0, "hh_z")
    iota(T["ip"][:], [[0, 1]], 0, 1, "ip")
    op("g", lambda e: e.affine_select(T["ident"][:], T["half"][:], [[-1, 128]], A.is_equal, 0.0, 0, 1),
       ["half"], ["ident"])
    op("v", None, ["ct_b", "hh_z"], [])
    quant("c0", T["ct"][:], ["ct_a", "ct_b"])
    send(("cc", "cs"), 0, ["c0"], "sent0")
    dma("y", T["wt"][:], T.w[:], ["sent0"], ["wt"])

    iota(T["ip4"][:], [[0, 1]], 0, 4, "ip4", grp="io1")
    iota(T["pa"][:], [[1, 4], [0, 2]], 0, 4, "pa", grp="io1")
    iota(T["ab"][:], [[0, 4], [-512, 8]], 127 * 256, 0, "ab", True, "io1")
    iota(T["zr"][:], [[0, 40]], 0, 0, "zr", True, "io1")
    iota(T["im"][:], [[1, 48]], 128, -1, "im", grp="io2")
    iota(T["ra"][:], [[4, 8], [4, 5]], 28 - 4 * r, 0, "ra", grp="io2")
    iota(T["rb"][:], [[0, 8], [1, 5]], 11, 0, "rb", grp="io2")
    iota(T["rc"][:], [[1, 8]], 48, 0, "rc", grp="io2")
    cut = min(G, r + 1)
    iota(T["kt"][:, 0:cut], [[512, cut]], 256 * (127 - 2 * r), 0, "kt0", True, "io3")
    if cut < G:
        iota(T["kt"][:, cut:G], [[512, G - cut]], 256 * (127 - 2 * (M - 1)), 0, "kt1", True, "io3")
    iota(T["land0"][:, 16:80], [[0, 64]], 0, 0, "lz0", True, "io3")

    ts(T["ja"][:], T["ip"][:], 15, None, A.bitwise_and, None, ["ip"], ["ja"])
    memset(T["one"][:], 0.0, "one")
    cp(T["l16"][:, 0:1], T["ja"][:], ["ja"], ["l16"])
    quant("x", T["xt"][:], ["xt"])
    cp(T["hh"][:, 16:20], T["ut"][:, 0:4], ["ut", "hh_z"], ["hh_u"])
    op("v", lambda e: e.memset(T["one"][:, 0:512:129], 1.0), ["one"], ["one0"], "fill1")
    op("v", lambda e: e.memset(T["one"][:, 7:512:127], 1.0), ["one"], ["one1"], "fill1")
    pickq("ca", C * r, C, "c0", 0, C, T["l16"][:, 0:1], ["l16", "c0"], ["ca_q"])
    picks("ca", C * r, C, "c0", 0, C, T["l16"][:, 0:1], ["l16", "c0"], ["ca_s"])
    quant("hi", T["hh"][:], ["hh_z", "hh_u"])
    mm("pz", "x", 0, "hi", 0, ["x", "hi"])
    quant("on", T["one"][:], ["one", "one0", "one1"])
    memset(T["ind"][:, 128:512], 0.0, "ind_z", "fill2")
    memset(T["row"][:, 40:48], 0.0, "row_z", "fill2")
    op("v", lambda e: e.tensor_reduce(T["mcol"][:, 0:1], T["pz"][:, 4:5], X, A.max), ["pz"], ["m0"])
    ts(T["ia"][:], T["ip"][:], 5, None, A.logical_shift_right, None, ["ip"], ["ia"], "c1")
    ts(T["ib"][:], T["ip4"][:], 127, None, A.bitwise_and, None, ["ip4"], ["ib"], "c1")
    ts(T["pb"][:], T["pa"][:], 63, None, A.bitwise_and, None, ["pa"], ["pb"], "c1")
    tt(T["idf"][:, 0:1], T["ib"][:], T["ia"][:], A.add, ["ia", "ib"], ["idf0"], "c2")
    tt(T["idf"][:, 1:2], T["ib"][:], T["ia"][:], A.subtract, ["ia", "ib"], ["idf1"], "c2")
    ts(T["pl"][:, 0:8:2], T["pb"][:, 0:8:2], 0.0, None, A.add, None, ["pb"], ["pl0"], "c2")
    ts(T["pl"][:, 1:8:2], T["pb"][:, 1:8:2], 64.0, None, A.add, None, ["pb"], ["pl1"], "c2")
    ts(T["tiep"][:, 0:1], T["idf"][:, 0:1], -1.0 / 128, 127.0 / 128, A.mult, A.add, ["idf0"], ["tiep"], "c3")
    ts(T["tiep"][:, 1:2], T["idf"][:, 1:2], -1.0 / 128, 124.0 / 128, A.mult, A.add, ["idf1"], ["tiep1"], "c3")
    ts(T["aa"][:], T["ab"][:], T["idf"][:, 0:1], None, A.add, None, ["ab", "idf0"], ["aa_z"], "c3")
    ts(T["imb"][:], T["im"][:], 15, None, A.bitwise_and, None, ["im"], ["imb"], "c4")
    ts(T["ra2"][:], T["ra"][:], 31, None, A.bitwise_and, None, ["ra"], ["ra2"], "c4")
    ts(T["m48"][:], T["imb"][:], 0.0, None, A.is_equal, None, ["imb"], ["m48"], "c5")
    tt(T["row"][:, 0:40], T["ra2"][:], T["rb"][:], A.add, ["ra2", "rb"], ["row"], "c5")
    for b in range(4):
        for k in range(4):
            op("s", lambda e, b=b, k=k: e.activation(T["ee"][:, 512 * b + k:512 * b + 512:4], T["ident"][:], ACT.Copy,
                                                     scale=1.0 if k == b else 0.0),
               ["ident"], ["ee%d" % (4 * b + k)], "ee")
    op("t", None, ["on", "ca_q", "ca_s"], [])
    op("v", None, ["m0", "tiep", "zr", "row", "pl0", "ind_z"], [])

    arrive("cc0")
    arrive("cs0")
    mm("pst", "x", 0, "ca", 0, ["x", "ca_q", "ca_s", "cc0", "cs0"])

    hkeys = ["hh_z", "hh_u"]
    mbk = ["mb0", "mb1", "mb2", "mb3"]
    for t in range(R):
        m = T["mcol"][:, t:t + 1]
        mk_, msg, off = "m%d" % t, T["msg%d" % t], T["off%d" % t][:, 0:1]
        op("s", lambda e, m=m: e.activation(T["m32"][:], T["zr"][:, 0:32], ACT.Identity, bias=m), ["zr", mk_], ["m32"])
        ts(T["ind"][:, 0:128], T["pst"][:, 0:128], m, None, A.is_gt, None, ["pst", mk_], ["ind"])
        quant("i%d" % t, T["ind"][:], ["ind", "ind_z"])
        mm("pcn", "on", 0, "i%d" % t, 0, ["on", "i%d" % t])
        for b in range(4):
            if b == 2:
                tr(msg[:], T["pcn"][:, 0:32], ["pcn"], ["msg%d" % t])
                send(("ga",), t, ["msg%d" % t])
            tr(T["mb"][0:32, 32 * b:32 * b + 32], T["m32"][32 * b:32 * b + 32, :], ["m32"], ["mb%d" % b], "mb%d" % t)
        if t == 0:
            pickq("cb", 0, 128, "ca", 0, 128, T["pl"][:, 0:8], ["pl0", "pl1", "ca_q", "cc0"], ["cbq"])
            picks("cb", 0, 128, "ca", 0, 128, T["pl"][:, 0:8], ["pl0", "pl1", "ca_s", "cs0"], ["cbs"])
            mm("psa", "cb", 0, "x", 0, ["x", "cbq", "cbs"])
        tt(T["init"][:], msg[:, 0:2], T["tiep"][:], A.add, ["msg%d" % t, "tiep", "tiep1"], ["init"])
        op("s", lambda e: e.activation(T["mb"][64:96, :], T["mb"][0:32, :], ACT.Copy), mbk, ["mbc"], "mc%d" % t)
        cp(T["mb"][32:64, :], T["mb"][0:32, :], mbk, ["mbb"], "mc%d" % t)
        cp(T["mb"][96:128, :], T["mb"][0:32, :], mbk, ["mbd"], "mc%d" % t)
        tt(T["df"][:], T["psa"][:, 0:128], T["mb"][:], A.subtract, ["psa", "mbb", "mbc", "mbd"] + mbk, ["df"])
        op("v", lambda e: e.tensor_tensor_scan(T["rm"][:], T["df"][:], T["df"][:], T["df"][:, 0:1], A.max, A.max),
           ["df"], ["rm"])
        op("s", lambda e, t=t: e.activation(T["junk"][:], T["rm"][:], ACT.Sign, bias=T["rm"][:, 127:128], scale=-1.0,
                                            accum_out=T["nm"][:, t:t + 1]), ["rm"], ["nm%d" % t, "junk"])
        if t == 0:
            quant("e", T["ee"][:], ["ee%d" % k for k in range(16)], 512)
        op("v", None, ["init", "lz%d" % t, "rm", "kt0"], [])
        op("s", None, ["nm%d" % t], [])
        arrive("ga%d" % t)
        land = T["land%d" % t]
        for c, out in enumerate((T["xx"][:, 26:64], T["xx"][:, 101:63:-1])):
            op("v", lambda e, c=c, land=land, out=out: e.tensor_tensor_scan(
                out, land[:, 2 + c:78:2], T["zr"][:, 0:38], T["init"][:, c:c + 1],
                A.add, A.add), ["ga%d" % t, "lz%d" % t, "zr", "init"], ["xx%d" % c], "xx%d" % t)
        tr(T["yy"][:, 0:64], T["xx"][:, 32:96], ["xx0", "xx1"], ["yy0"], "yy%d" % t)
        tr(T["yy"][0:64, 64:128], T["xx"][64:128, 32:96], ["xx0", "xx1"], ["yy1"], "yy%d" % t)
        tr(T["yy"][64:128, 64:128], T["xx"][0:64, 32:96], ["xx0", "xx1"], ["yy2"], "yy%d" % t)
        rank_of(0)
        for j in range(2):
            ts(T["aa"][:, 16 * j + 12:16 * j + 16], T["kt"][:], T["nm"][:, t:t + 1], None, A.add, None,
               ["kt0", "nm%d" % t, "aa_z"], ["aa%d" % j], "aa%d" % t)
        op("v", None, ["aa0"], [])
        ts(T["x2"][:], T["aa"][:], 1.0 / 256, T["rk"][:, 0:1], A.mult, A.subtract, ["aa_z", "aa0", "aa1", "rk0"], ["x2"])
        tr(T["y2"][0:64, 0:32], T["x2"][0:64, :], ["x2"], ["y2a"], "y2%d" % t)
        tr(T["y2"][0:64, 32:64], T["x2"][64:128, :], ["x2"], ["y2b"], "y2%d" % t)
        op("v", lambda e, t=t: e.tensor_reduce(T["r1"][0:64, t:t + 1], T["y2"][0:64, :], X, A.min,
                                               apply_absolute_value=True), ["y2a", "y2b"], ["r1%d" % t])
        for a in range(4):
            ts(T["off%d" % t][32 * a:32 * a + 32, 0:1], T["r1"][0:32, t:t + 1], T["r1"][32:64, t:t + 1], 256.0,
               A.min, A.mult, ["r1%d" % t], ["off%d_%d" % (t, a)], "off%d" % t)
        offk = ["off%d_%d" % (t, a) for a in range(4)]
        sn, tk = "sn%d" % t, "tk%d" % t
        pickq(sn, 0, 16, "x", 0, 128, off, offk + ["x"], [sn + "q"])
        picks(sn, 0, 16, "x", 0, 128, off, offk + ["x"], [sn + "s"])
        send(("tc", "ts"), t, [sn + "q", sn + "s"], "sentl" if t == R - 1 else "sent")
        if t < R - 1:
            rank_of(1)
            iota(T["land%d" % (t + 1)][:, 16:80], [[0, 64]], 0, 0, "lz%d" % (t + 1), True)
        pickq(tk, 0, 16, "x", 0, 128, off, offk + ["x"], [tk + "q0"])
        picks(tk, 0, 16, "x", 0, 128, off, offk + ["x"], [tk + "s0"])
        pickq(tk, 48, 16, "ca", 0, 128, off, offk + ["ca_q", "cc0"], [tk + "q1"])
        picks(tk, 48, 16, "ca", 0, 128, off, offk + ["ca_s", "cs0"], [tk + "s1"])
        if t == 0:
            cp(T["row"][:, 0:40:5], T["rc"][:], ["rc"], ["row"])
            memset(T["mult"][:], 0.5, "mult")
        ts(T["lf"][0:32, t:t + 1], T["r1"][0:32, t:t + 1], T["r1"][32:64, t:t + 1], 256.0, A.min, A.mult,
           ["r1%d" % t], ["lf%d" % t])
        if t == 0:
            tt(T["pr"][:], T["row"][:], T["m48"][:], A.mult, ["row", "row_z", "m48"], ["pr"])
            op("v", lambda e: e.memset(T["mult"][:, 0:40:5], 0.0), ["mult"], ["mult0"], "mu")
            op("v", lambda e: e.memset(T["mult"][:, 1:40:5], 1.0), ["mult"], ["mult1"], "mu")
            for c in range(3):
                op("v", lambda e, c=c: e.tensor_reduce(T["l3"][:, c:c + 1], T["pr"][:, 16 * c:16 * c + 16], X, A.add),
                   ["pr"], ["l3%d" % c], "l3")
        if t < R - 1:
            ts(T["pen"][:], T["rk"][:], 112.0, -2048.0, A.is_gt, A.mult, ["rk0", "rk1"], ["pen"])
        if t == 0:
            cp(T["lst"][:, 0:3], T["l3"][:, 0:3], ["l30", "l31", "l32"], ["lst"])
            quant("mv", T["xt"][:], ["xt"], 128, 48, "mvf")
        if t == 1:
            ts(T["jb"][:], T["ja"][:], 7.0, 5.0, A.min, A.mult, ["ja"], ["jb"])
            ts(T["olst"][:, 0:1], T["ja"][:], 5.0, 9.0, A.mult, A.add, ["ja"], ["ol0"])
        if t < R - 1:
            tt(T["tiep"][:], T["tiep"][:], T["pen"][:], A.add, ["pen", "tiep", "tiep1"], ["tiep"])
        if t == 1:
            ts(T["olst"][:, 1:2], T["jb"][:], 89.0, None, A.add, None, ["jb"], ["ol1"])
        if t == R - 1:
            quant("w", T["wt"][:], ["wt"], 256)
            for k in range(R):
                dma("y", T.sel[0:1, M * k:M * k + M], T["lf"][0:M, k:k + 1], ["lf%d" % k, "sentl"], ["o_sel%d" % k],
                    "osel")
        late = ["ol0", "ol1", "w"] if t == R - 1 else []
        op("v", None, ["lst", tk + "q0", tk + "q1", "tiep", "mult0", "mvf"] + late, [])
        op("s", None, ["lst", tk + "s0", tk + "s1"] + late[:2], [])
        op("t", None, ["mvf", "e"] + late[2:], [])
        arrive("tc%d" % t)
        arrive("ts%d" % t)
        pa = (0, 176, 224)[t]
        va = (0, 96, 144)[t]
        pickq("mv", pa, 48, tk, 0, 64, T["lst"][:, 0:3], ["lst", tk + "q0", tk + "q1", "tc%d" % t], ["mvq%d" % t])
        picks("mv", pa, 48, tk, 0, 64, T["lst"][:, 0:3], ["lst", tk + "s0", tk + "s1", "ts%d" % t], ["mvs%d" % t])
        mvk = ["mvf", "e", "mvq%d" % t, "mvs%d" % t] + (["mvq1", "mvs1"] if t == 2 else [])
        for b in range(4):
            mm("pd%d" % b, "e", 128 * b, "mv", va, mvk)
        h0 = 4 * (5 + 40 * t)
        for b in range(4):
            op("v", lambda e, b=b, h0=h0, k=pa - va: e.tensor_tensor_scan(
                T["hh"][:, h0 + b:h0 + 160:4], T["mult"][:], T["pd%d" % b][:, k:k + 40], 0.0, A.mult, A.add),
               ["pd%d" % b, "mult0", "mult1", "hh_z", "hi" if t == 0 else "h%d" % (t - 1)], ["hh%d_%d" % (t, b)],
               "hv%d" % t)
            hkeys.append("hh%d_%d" % (t, b))
        quant("h%d" % t, T["hh"][:], hkeys)
        mm("pz", "x", 0, "h%d" % t, 0, ["x", "h%d" % t])
        if t == R - 1:
            mm("pcn", "w", 0, "h2", 0, ["w", "h2"])
            mm("psa", "w", 128, "h2", 0, ["w", "h2"])
            pickq("o", 0, 32, "h2", 0, 128, T["olst"][:, 0:2], ["ol0", "ol1", "h2"], ["oq"])
            picks("o", 0, 32, "h2", 0, 128, T["olst"][:, 0:2], ["ol0", "ol1", "h2"], ["os"])
        op("v", lambda e, t=t: e.tensor_reduce(T["mcol"][:, t + 1:t + 2], T["pz"][:, 4:5 + 40 * (t + 1):5], X, A.max),
           ["pz"], ["m%d" % (t + 1)])

    n = R * M
    cp(T["ys"][:, 0:n], T["pcn"][:, 9:125:5], ["pcn"], ["ys0"])
    cp(T["ys"][:, n:2 * n], T["psa"][:, 9:125:5], ["psa"], ["ys1"])
    dma("y", T.oc[:, 0:4 * n], _b8(T["oq"][:, 0:n]), ["oq"], ["o_oc"], "outy")
    for k in range(4):
        dma("y" if k < 2 else "s", T.osc[4 * k:4 * k + 4, 0:n], T["os"][32 * k:32 * k + 4, 0:n], ["os"],
            ["o_os%d" % k], "outy")
    dma("y", T.mk[0:1, :], T["mcol"][:, R:R + 1], ["m%d" % R], ["o_mk"], "outy")
    dma("s", T.y[:], T["ys"][:], ["ys0", "ys1"], ["o_y"], "outy")
    op("g", lambda e: e.wait_ge(T.sem["sent"], sent["sent"]), [], [], None, "remote")
    op("y", None, ["o_sel0", "o_oc"], [])
    _emit(g, T, ops)
